import numpy as np
import ml_dtypes


def mxq(x, axis, fmt="e4m3"):
    dtype, down = {"e4m3": (ml_dtypes.float8_e4m3fn, 7), "e5m2": (ml_dtypes.float8_e5m2, 14)}[fmt]
    v = np.moveaxis(np.asarray(x, np.float32).astype(ml_dtypes.bfloat16).astype(np.float64), axis, -1)
    blocks = v.reshape(v.shape[:-1] + (-1, 32))
    amax = np.abs(blocks).max(-1, keepdims=True)
    byte = np.maximum(np.where(amax > 0, np.frexp(amax)[1] - 1 + 127, 0) - down, 1)
    scale = np.exp2(byte - 127.0)
    codes = (blocks / scale).astype(np.float32).astype(dtype).astype(np.float64)
    return np.moveaxis((codes * scale).reshape(v.shape), -1, axis)


WIDE = False


def mx_kscale(k):
    if not WIDE:
        return np.ones(k)
    levels = np.array([10, -10, 5, -5, 0])
    if k % 512:
        return np.exp2(np.random.permutation(np.resize(levels, k // 32))).repeat(32)
    a = np.empty((k // 512, 16))
    for p in range(k // 512):
        a[p, :8] = np.random.permutation(np.resize(levels, 8))
        for g in range(8):
            far = levels[np.abs(levels - a[p, g]) >= 10]
            a[p, g + 8] = far[np.random.randint(len(far))]
    return np.exp2(a.ravel()).repeat(32)


def f64(x):
    return np.asarray(x).astype(np.float64)


def striped(idx):
    return np.tile(idx.reshape(-1, 16).T, (8, 1)).astype(np.uint16)


def unstriped(offs):
    return offs[:16].T.reshape(-1).astype(np.int64)


def pack_weight(w):
    k, n = w.shape
    w = f64(np.asarray(w, np.float32).astype(ml_dtypes.bfloat16)).reshape(k // 32, 32, n)
    amax = np.abs(w).max(1)
    byte = np.clip(np.where(amax > 0, np.frexp(amax)[1] - 1 + 127 - 7, 1), 1, 254)
    scaled = (w * np.exp2(127.0 - byte)[:, None, :]).reshape(k, n).astype(np.float32)
    words = np.ascontiguousarray(scaled.reshape(k // 512, 128, 4, n).transpose(0, 1, 3, 2)).astype(ml_dtypes.float8_e4m3fn).view(np.uint8)
    return words, np.ascontiguousarray(byte.astype(np.uint8).reshape(k // 512, 16, n))


def unpack_weight(words, scales):
    g, p, n, _ = words.shape
    vals = np.ascontiguousarray(words).view(ml_dtypes.float8_e4m3fn).astype(np.float64) * np.repeat(np.exp2(scales.astype(np.float64) - 127.0), 8, axis=1)[..., None]
    return vals.transpose(0, 1, 3, 2).reshape(g * 512, n)


def sigmoid(v):
    return 1.0 / (1.0 + np.exp(-np.maximum(v, -700.0)))


K, T, S, V = 1024, 2048, 1024, 512
P = 2 ** 7


def setup_inputs():
    n = np.random.standard_normal
    s = mx_kscale(K)[:, None]
    packed_xT = pack_weight(n((K, T)) * s)
    return {
        "x_words": packed_xT[0],
        "x_scales": packed_xT[1],
        "w1": (n((K, K)) / K / s / s.T).astype(np.float32),
        "ment": (np.tile(0.5 * np.random.standard_normal(T), (P, 1))).astype(np.float32),
        "offs": striped(np.random.permutation(T)[:S]),
        "ant": striped(np.random.permutation(T)[:V]),
    }


def reference(x_words, x_scales, w1, ment, offs, ant):
    xq = unpack_weight(x_words, x_scales)[:, unstriped(offs)]
    z = mxq(f64(w1), 0, "e4m3").T @ xq
    x_ant = unpack_weight(x_words, x_scales)[:, unstriped(ant)]
    y = (mxq(z, 0, "e4m3").T @ x_ant) + f64(ment)[:1][:, unstriped(ant)]
    return sigmoid(y)

@@ -1,0 +1,190 @@
+from contextlib import ExitStack
+
+import concourse.mybir as mybir
+
+K, T, S, V = 1024, 2048, 1024, 512
+FLOPS = 2 * K * K * S + 2 * K * S * V
+
+F32 = mybir.dt.float32
+BF16 = mybir.dt.bfloat16
+I32 = mybir.dt.int32
+U32 = mybir.dt.uint32
+U16 = mybir.dt.uint16
+U8 = mybir.dt.uint8
+FP8X4 = mybir.dt.float8_e4m3fn_x4
+SIGMOID = mybir.ActivationFunctionType.Sigmoid
+ADD = mybir.AluOpType.add
+
+P = 128
+PACK = 4
+K_PASS = P * PACK
+PASSES = K // K_PASS
+BLOCKS = S // P
+LIST_COL = 16
+HALF = P // 2
+LAG = 5
+
+
+def tile_picked_zcoref_sig_p_kernel(tc, x_words, x_scales, w1, ment, offs, ant, out):
+    nc = tc.nc
+    with ExitStack() as ctx:
+        keep = ctx.enter_context(tc.tile_pool(name="keep", bufs=1))
+        ring = ctx.enter_context(tc.tile_pool(name="ring", bufs=8))
+        psum = ctx.enter_context(tc.psum_pool(name="psum", bufs=8))
+
+        offs_sb = keep.tile([P, S // LIST_COL], U16, name="offs_sb")
+        ant_sb = keep.tile([P, V // LIST_COL], U16, name="ant_sb")
+        scale_win = keep.tile([P, T], U8, name="scale_win", align_bytes=64)
+        word_win = [keep.tile([P, T], I32, name=f"word_win{o}", align_bytes=64) for o in range(PASSES)]
+        ment_win = keep.tile([P, T], F32, name="ment_win", align_bytes=64)
+        w_raw = {(o, h): keep.tile([P, PACK, K_PASS], F32, name=f"w_raw{o}{h}", align_bytes=64)
+                 for o in range(PASSES) for h in range(PASSES)}
+
+        warm = keep.tile([P, 2], F32, name="warm")
+        nc.gpsimd.memset(warm[:, 0:1], 0.0)
+        nc.scalar.activation(warm[:, 1:2], warm[:, 0:1], SIGMOID)
+
+        nc.vector.memset(scale_win[:].bitcast(I32), 0)
+        nc.sync.dma_start(offs_sb[:], offs)
+        for q in range(4):
+            nc.sync.dma_start(
+                scale_win[32 * q : 32 * q + 4 * PASSES, :].bitcast(I32),
+                x_scales[:, 4 * q : 4 * q + 4, :].bitcast(I32),
+            )
+
+        def load_w(o, h, first=0, last=P):
+            rows = w1[o * K_PASS : (o + 1) * K_PASS, h * K_PASS + PACK * first : h * K_PASS + PACK * last]
+            nc.sync.dma_start(w_raw[o, h][:, :, PACK * first : PACK * last], rows.rearrange("(p j) c -> p j c", j=PACK))
+
+        def load_x(o):
+            nc.sync.dma_start(word_win[o][:], x_words[o].rearrange("p n t -> p (n t)").bitcast(I32))
+
+        nc.sync.dma_start(ant_sb[:], ant)
+        for o in range(PASSES):
+            load_w(o, 0, 0, HALF)
+            load_w(o, 0, HALF, P)
+            load_x(o)
+        for o in range(PASSES):
+            load_w(o, 1, 0, HALF)
+            load_w(o, 1, HALF, P)
+        nc.sync.dma_start(ment_win[:], ment)
+
+        span_words = [keep.tile([P, S], U32, name=f"span_words{o}", align_bytes=64) for o in range(PASSES)]
+        span_scales = keep.tile([P, S], U8, name="span_scales", align_bytes=64)
+        ant_words = [keep.tile([P, V], U32, name=f"ant_words{o}", align_bytes=64) for o in range(PASSES)]
+        ant_scales = keep.tile([P, V], U8, name="ant_scales", align_bytes=64)
+        ant_ment = keep.tile([P, V], F32, name="ant_ment", align_bytes=64)
+
+        def gather_span_words(o, first, last):
+            cols = offs_sb[:, first // LIST_COL : last // LIST_COL]
+            nc.vector.tensor_copy(span_words[o][:, first:last], word_win[o][:].bitcast(U32).indirect(cols))
+
+        def gather_ant_words(o):
+            nc.vector.tensor_copy(ant_words[o][:], word_win[o][:].bitcast(U32).indirect(ant_sb[:]))
+
+        w_bf = {key: keep.tile([P, PACK, P, PACK], BF16, name=f"w_bf{key[0]}{key[1]}", align_bytes=64) for key in w_raw}
+        w_codes = {key: keep.tile([P, K_PASS], U32, name=f"w_codes{key[0]}{key[1]}", align_bytes=64) for key in w_raw}
+        w_scales = {key: keep.tile([P, K_PASS], U8, name=f"w_scales{key[0]}{key[1]}", align_bytes=64) for key in w_raw}
+
+        def round_w(copy, o, h, first, last):
+            copy(
+                w_bf[o, h][:, :, first:last, :].rearrange("p t m j -> p m j t"),
+                w_raw[o, h][:, :, PACK * first : PACK * last].rearrange("p j (m t) -> p m j t", t=PACK),
+            )
+
+        def quantize_w(o, h):
+            nc.vector.quantize_mx(
+                out=w_codes[o, h][:].bitcast(FP8X4),
+                scales=w_scales[o, h][:],
+                in_=w_bf[o, h][:].rearrange("p t m j -> p (t m j)"),
+            )
+
+        z_codes = [keep.tile([P, S], U32, name=f"z_codes{h}", align_bytes=64) for h in range(PASSES)]
+        z_scales = [keep.tile([P, S], U8, name=f"z_scales{h}", align_bytes=64) for h in range(PASSES)]
+        z_bank = {}
+
+        def z_pass(h, b, o):
+            if o == 0:
+                z_bank[h, b] = psum.tile([P, PACK, P], F32, name="bank", tag="bank")
+            spans = slice(b * P, (b + 1) * P)
+            for t in range(PACK):
+                cols = slice(t * P, (t + 1) * P)
+                nc.tensor.matmul_mx(
+                    out=z_bank[h, b][:, t, :],
+                    lhsT=w_codes[o, h][:, cols].bitcast(FP8X4),
+                    lhsT_scale=w_scales[o, h][:, cols],
+                    rhs=span_words[o][:, spans].bitcast(FP8X4),
+                    rhs_scale=span_scales[4 * o :, spans],
+                    start=(o == 0 and t == 0),
+                    stop=(o == PASSES - 1 and t == PACK - 1),
+                )
+
+        z_bf = [keep.tile([P, S, PACK], BF16, name=f"z_bf{h}", align_bytes=64) for h in range(PASSES)]
+
+        def round_z(h, b):
+            nc.scalar.copy(z_bf[h][:, b * P : (b + 1) * P, :], z_bank[h, b][:].rearrange("p t n -> p n t"))
+
+        def quantize_z(h, first, last):
+            spans = slice(first * P, last * P)
+            nc.vector.quantize_mx(
+                out=z_codes[h][:, spans].bitcast(FP8X4),
+                scales=z_scales[h][:, spans],
+                in_=z_bf[h][:, spans, :].rearrange("p n t -> p (n t)"),
+            )
+
+        def score(b):
+            spans = slice(b * P, (b + 1) * P)
+            y_bank = psum.tile([P, V], F32, name="bank", tag="bank")
+            for h in range(PASSES):
+                nc.tensor.matmul_mx(
+                    out=y_bank[:],
+                    lhsT=z_codes[h][:, spans].bitcast(FP8X4),
+                    lhsT_scale=z_scales[h][:, spans],
+                    rhs=ant_words[h][:].bitcast(FP8X4),
+                    rhs_scale=ant_scales[4 * h :, :],
+                    start=(h == 0),
+                    stop=(h == PASSES - 1),
+                )
+            logit = ring.tile([P, V], F32, name="logit", tag="logit")
+            nc.vector.tensor_tensor(logit[:], y_bank[:], ant_ment[:], ADD)
+            prob = ring.tile([P, V], F32, name="prob", tag="prob")
+            nc.scalar.activation(prob[:], logit[:], SIGMOID)
+            nc.sync.dma_start(out[spans, :], prob[:])
+
+        nc.vector.tensor_copy(span_scales[:], scale_win[:].indirect(offs_sb[:]))
+        nc.vector.tensor_copy(ant_scales[:], scale_win[:].indirect(ant_sb[:]))
+        round_w(nc.scalar.copy, 0, 0, 0, HALF)
+        round_w(nc.scalar.copy, 0, 0, HALF, P)
+        gather_span_words(0, 0, S // 2)
+        quantize_w(0, 0)
+        gather_span_words(0, S // 2, S)
+        for b in range(BLOCKS):
+            z_pass(0, b, 0)
+        round_w(nc.scalar.copy, 1, 0, 0, HALF)
+        round_w(nc.scalar.copy, 1, 0, HALF, P)
+        quantize_w(1, 0)
+        gather_span_words(1, 0, S // 4)
+        gather_span_words(1, S // 4, S // 2)
+        gather_span_words(1, S // 2, S)
+        round_w(nc.scalar.copy, 0, 1, 0, HALF)
+        round_w(nc.scalar.copy, 0, 1, HALF, P)
+        quantize_w(0, 1)
+        round_w(nc.vector.tensor_copy, 1, 1, 0, P)
+        quantize_w(1, 1)
+        for b in range(BLOCKS):
+            z_pass(0, b, 1)
+            round_z(0, b)
+            if b % 4 == 3:
+                quantize_z(0, b - 3, b + 1)
+        for b in range(BLOCKS):
+            z_pass(1, b, 0)
+        gather_ant_words(0)
+        gather_ant_words(1)
+        nc.vector.tensor_copy(ant_ment[:], ment_win[:].indirect(ant_sb[:]))
+        for b in range(BLOCKS + LAG):
+            if b < BLOCKS:
+                z_pass(1, b, 1)
+                round_z(1, b)
+                quantize_z(1, b, b + 1)
+            if b >= LAG:
+                score(b - LAG)

@@ -19,172 +19,190 @@ P = 128
 PACK = 4
 K_PASS = P * PACK
 PASSES = K // K_PASS
-BLOCKS = S // P
+QUADRANTS = 4
+QUADRANT = P // QUADRANTS
+SCALE_ROWS = 4
 LIST_COL = 16
+BLOCKS = S // P
+BANKS = 8
 HALF = P // 2
-LAG = 5
+VECTOR_SHARE = HALF // 2
+Z_GROUP = 4
 
 
 def tile_picked_zcoref_sig_p_kernel(tc, x_words, x_scales, w1, ment, offs, ant, out):
     nc = tc.nc
     with ExitStack() as ctx:
         keep = ctx.enter_context(tc.tile_pool(name="keep", bufs=1))
-        ring = ctx.enter_context(tc.tile_pool(name="ring", bufs=8))
-        psum = ctx.enter_context(tc.psum_pool(name="psum", bufs=8))
+        ring = ctx.enter_context(tc.tile_pool(name="ring", bufs=BLOCKS))
+        reuse = ctx.enter_context(tc.tile_pool(name="reuse", bufs=1))
+        psum = ctx.enter_context(tc.psum_pool(name="psum", bufs=BANKS))
 
         offs_sb = keep.tile([P, S // LIST_COL], U16, name="offs_sb")
         ant_sb = keep.tile([P, V // LIST_COL], U16, name="ant_sb")
         scale_win = keep.tile([P, T], U8, name="scale_win", align_bytes=64)
         word_win = [keep.tile([P, T], I32, name=f"word_win{o}", align_bytes=64) for o in range(PASSES)]
         ment_win = keep.tile([P, T], F32, name="ment_win", align_bytes=64)
-        w_raw = {(o, h): keep.tile([P, PACK, K_PASS], F32, name=f"w_raw{o}{h}", align_bytes=64)
-                 for o in range(PASSES) for h in range(PASSES)}
 
         warm = keep.tile([P, 2], F32, name="warm")
         nc.gpsimd.memset(warm[:, 0:1], 0.0)
         nc.scalar.activation(warm[:, 1:2], warm[:, 0:1], SIGMOID)
 
         nc.vector.memset(scale_win[:].bitcast(I32), 0)
-        nc.sync.dma_start(offs_sb[:], offs)
-        for q in range(4):
-            nc.sync.dma_start(
-                scale_win[32 * q : 32 * q + 4 * PASSES, :].bitcast(I32),
-                x_scales[:, 4 * q : 4 * q + 4, :].bitcast(I32),
-            )
 
-        def load_w(o, h, first=0, last=P):
+        w_raw = {}
+
+        def load_w(o, h, first, last):
+            w_raw[o, h, first] = keep.tile([P, PACK, PACK * (last - first)], F32, name=f"w_raw{o}{h}_{first}", align_bytes=64)
             rows = w1[o * K_PASS : (o + 1) * K_PASS, h * K_PASS + PACK * first : h * K_PASS + PACK * last]
-            nc.sync.dma_start(w_raw[o, h][:, :, PACK * first : PACK * last], rows.rearrange("(p j) c -> p j c", j=PACK))
+            nc.sync.dma_start(w_raw[o, h, first][:], rows.rearrange("(p j) c -> p j c", j=PACK))
 
         def load_x(o):
-            nc.sync.dma_start(word_win[o][:], x_words[o].rearrange("p n t -> p (n t)").bitcast(I32))
+            nc.sync.dma_start(word_win[o][:], x_words[o].rearrange("p n r -> p (n r)").bitcast(I32))
 
+        load_w(0, 0, 0, HALF)
+        nc.sync.dma_start(offs_sb[:], offs)
+        for q in range(QUADRANTS):
+            nc.sync.dma_start(
+                scale_win[QUADRANT * q : QUADRANT * q + SCALE_ROWS * PASSES, :].bitcast(I32),
+                x_scales[:, SCALE_ROWS * q : SCALE_ROWS * (q + 1), :].bitcast(I32),
+            )
         nc.sync.dma_start(ant_sb[:], ant)
-        for o in range(PASSES):
-            load_w(o, 0, 0, HALF)
-            load_w(o, 0, HALF, P)
-            load_x(o)
-        for o in range(PASSES):
-            load_w(o, 1, 0, HALF)
-            load_w(o, 1, HALF, P)
+        load_w(0, 0, HALF, P)
+        load_x(0)
+        load_w(1, 0, 0, HALF)
+        load_w(1, 0, HALF, P)
+        load_x(1)
+        load_w(0, 1, 0, HALF)
+        load_w(0, 1, HALF, P)
+        load_w(1, 1, 0, P)
         nc.sync.dma_start(ment_win[:], ment)
 
+        blocks = [(o, h) for h in range(PASSES) for o in range(PASSES)]
+        w_codes = {(o, h): keep.tile([P, K_PASS], U32, name=f"w_codes{o}{h}", align_bytes=64) for o, h in blocks}
+        w_scales = {(o, h): keep.tile([P, K_PASS], U8, name=f"w_scales{o}{h}", align_bytes=64) for o, h in blocks}
+        w_bf = {(o, h): keep.tile([P, PACK, P, PACK], BF16, name=f"w_bf{o}{h}", align_bytes=64) for o, h in blocks[:-1]}
         span_words = [keep.tile([P, S], U32, name=f"span_words{o}", align_bytes=64) for o in range(PASSES)]
         span_scales = keep.tile([P, S], U8, name="span_scales", align_bytes=64)
         ant_words = [keep.tile([P, V], U32, name=f"ant_words{o}", align_bytes=64) for o in range(PASSES)]
         ant_scales = keep.tile([P, V], U8, name="ant_scales", align_bytes=64)
-        ant_ment = keep.tile([P, V], F32, name="ant_ment", align_bytes=64)
+        z_codes = [keep.tile([P, S], U32, name=f"z_codes{h}", align_bytes=64) for h in range(PASSES)]
+
+        w_bf[1, 1] = reuse.tile([P, PACK, P, PACK], BF16, name="w_bf11", align_bytes=64, offset=0)
+        z_scales = [
+            reuse.tile([P, S], U8, name="z_scales0", align_bytes=64, offset=0),
+            keep.tile([P, S], U8, name="z_scales1", align_bytes=64),
+        ]
+        ant_ment = reuse.tile([P, V], F32, name="ant_ment", align_bytes=64, offset=S)
+
+        z_bf = [
+            keep.tile([P, S, PACK], BF16, name="z_bf0", tag=f"w_raw01_{HALF}", align_bytes=64),
+            keep.tile([P, S, PACK], BF16, name="z_bf1", align_bytes=64),
+        ]
+        z_bank = {}
 
         def gather_span_words(o, first, last):
-            cols = offs_sb[:, first // LIST_COL : last // LIST_COL]
-            nc.vector.tensor_copy(span_words[o][:, first:last], word_win[o][:].bitcast(U32).indirect(cols))
+            entries = offs_sb[:, first // LIST_COL : last // LIST_COL]
+            nc.vector.tensor_copy(span_words[o][:, first:last], word_win[o][:].bitcast(U32).indirect(entries))
 
-        def gather_ant_words(o):
-            nc.vector.tensor_copy(ant_words[o][:], word_win[o][:].bitcast(U32).indirect(ant_sb[:]))
-
-        w_bf = {key: keep.tile([P, PACK, P, PACK], BF16, name=f"w_bf{key[0]}{key[1]}", align_bytes=64) for key in w_raw}
-        w_codes = {key: keep.tile([P, K_PASS], U32, name=f"w_codes{key[0]}{key[1]}", align_bytes=64) for key in w_raw}
-        w_scales = {key: keep.tile([P, K_PASS], U8, name=f"w_scales{key[0]}{key[1]}", align_bytes=64) for key in w_raw}
-
-        def round_w(copy, o, h, first, last):
+        def round_w(copy, o, h, piece, first, last):
+            cols = slice(PACK * (first - piece), PACK * (last - piece))
             copy(
-                w_bf[o, h][:, :, first:last, :].rearrange("p t m j -> p m j t"),
-                w_raw[o, h][:, :, PACK * first : PACK * last].rearrange("p j (m t) -> p m j t", t=PACK),
+                w_bf[o, h][:, :, first:last, :].rearrange("p r m j -> p m j r"),
+                w_raw[o, h, piece][:, :, cols].rearrange("p j (m r) -> p m j r", r=PACK),
             )
 
         def quantize_w(o, h):
             nc.vector.quantize_mx(
                 out=w_codes[o, h][:].bitcast(FP8X4),
                 scales=w_scales[o, h][:],
-                in_=w_bf[o, h][:].rearrange("p t m j -> p (t m j)"),
+                in_=w_bf[o, h][:].rearrange("p r m j -> p (r m j)"),
             )
-
-        z_codes = [keep.tile([P, S], U32, name=f"z_codes{h}", align_bytes=64) for h in range(PASSES)]
-        z_scales = [keep.tile([P, S], U8, name=f"z_scales{h}", align_bytes=64) for h in range(PASSES)]
-        z_bank = {}
 
         def z_pass(h, b, o):
             if o == 0:
-                z_bank[h, b] = psum.tile([P, PACK, P], F32, name="bank", tag="bank")
+                z_bank[h, b] = psum.tile([P, PACK, P], F32, name="z_bank", tag="bank")
             spans = slice(b * P, (b + 1) * P)
-            for t in range(PACK):
-                cols = slice(t * P, (t + 1) * P)
+            for r in range(PACK):
+                places = slice(r * P, (r + 1) * P)
                 nc.tensor.matmul_mx(
-                    out=z_bank[h, b][:, t, :],
-                    lhsT=w_codes[o, h][:, cols].bitcast(FP8X4),
-                    lhsT_scale=w_scales[o, h][:, cols],
+                    out=z_bank[h, b][:, r, :],
+                    lhsT=w_codes[o, h][:, places].bitcast(FP8X4),
+                    lhsT_scale=w_scales[o, h][:, places],
                     rhs=span_words[o][:, spans].bitcast(FP8X4),
-                    rhs_scale=span_scales[4 * o :, spans],
-                    start=(o == 0 and t == 0),
-                    stop=(o == PASSES - 1 and t == PACK - 1),
+                    rhs_scale=span_scales[SCALE_ROWS * o :, spans],
+                    start=(o == 0 and r == 0),
+                    stop=(o == PASSES - 1 and r == PACK - 1),
                 )
 
-        z_bf = [keep.tile([P, S, PACK], BF16, name=f"z_bf{h}", align_bytes=64) for h in range(PASSES)]
-
         def round_z(h, b):
-            nc.scalar.copy(z_bf[h][:, b * P : (b + 1) * P, :], z_bank[h, b][:].rearrange("p t n -> p n t"))
+            nc.scalar.copy(z_bf[h][:, b * P : (b + 1) * P, :], z_bank[h, b][:].rearrange("p r n -> p n r"))
 
         def quantize_z(h, first, last):
             spans = slice(first * P, last * P)
             nc.vector.quantize_mx(
                 out=z_codes[h][:, spans].bitcast(FP8X4),
                 scales=z_scales[h][:, spans],
-                in_=z_bf[h][:, spans, :].rearrange("p n t -> p (n t)"),
+                in_=z_bf[h][:, spans, :].rearrange("p n r -> p (n r)"),
             )
 
         def score(b):
             spans = slice(b * P, (b + 1) * P)
-            y_bank = psum.tile([P, V], F32, name="bank", tag="bank")
+            y_bank = psum.tile([P, V], F32, name="y_bank", tag="bank")
             for h in range(PASSES):
                 nc.tensor.matmul_mx(
                     out=y_bank[:],
                     lhsT=z_codes[h][:, spans].bitcast(FP8X4),
                     lhsT_scale=z_scales[h][:, spans],
                     rhs=ant_words[h][:].bitcast(FP8X4),
-                    rhs_scale=ant_scales[4 * h :, :],
+                    rhs_scale=ant_scales[SCALE_ROWS * h :, :],
                     start=(h == 0),
                     stop=(h == PASSES - 1),
                 )
-            logit = ring.tile([P, V], F32, name="logit", tag="logit")
+            logit = ring.tile([P, V], F32, name="logit")
             nc.vector.tensor_tensor(logit[:], y_bank[:], ant_ment[:], ADD)
-            prob = ring.tile([P, V], F32, name="prob", tag="prob")
+            prob = ring.tile([P, V], F32, name="prob")
             nc.scalar.activation(prob[:], logit[:], SIGMOID)
             nc.sync.dma_start(out[spans, :], prob[:])
 
         nc.vector.tensor_copy(span_scales[:], scale_win[:].indirect(offs_sb[:]))
-        nc.vector.tensor_copy(ant_scales[:], scale_win[:].indirect(ant_sb[:]))
-        round_w(nc.scalar.copy, 0, 0, 0, HALF)
-        round_w(nc.scalar.copy, 0, 0, HALF, P)
         gather_span_words(0, 0, S // 2)
-        quantize_w(0, 0)
         gather_span_words(0, S // 2, S)
+        round_w(nc.scalar.copy, 0, 0, 0, 0, HALF)
+        round_w(nc.scalar.copy, 0, 0, HALF, HALF, P)
+        quantize_w(0, 0)
         for b in range(BLOCKS):
             z_pass(0, b, 0)
-        round_w(nc.scalar.copy, 1, 0, 0, HALF)
-        round_w(nc.scalar.copy, 1, 0, HALF, P)
+
+        round_w(nc.scalar.copy, 1, 0, 0, 0, HALF)
+        round_w(nc.scalar.copy, 1, 0, HALF, HALF, P)
         quantize_w(1, 0)
         gather_span_words(1, 0, S // 4)
         gather_span_words(1, S // 4, S // 2)
         gather_span_words(1, S // 2, S)
-        round_w(nc.scalar.copy, 0, 1, 0, HALF)
-        round_w(nc.scalar.copy, 0, 1, HALF, P)
+
+        round_w(nc.scalar.copy, 0, 1, 0, 0, HALF - VECTOR_SHARE)
+        round_w(nc.scalar.copy, 0, 1, HALF, HALF, P)
+        round_w(nc.vector.tensor_copy, 0, 1, 0, HALF - VECTOR_SHARE, HALF)
         quantize_w(0, 1)
-        round_w(nc.vector.tensor_copy, 1, 1, 0, P)
+        round_w(nc.vector.tensor_copy, 1, 1, 0, 0, P)
         quantize_w(1, 1)
+
         for b in range(BLOCKS):
             z_pass(0, b, 1)
             round_z(0, b)
-            if b % 4 == 3:
-                quantize_z(0, b - 3, b + 1)
+            if (b + 1) % Z_GROUP == 0:
+                quantize_z(0, b + 1 - Z_GROUP, b + 1)
+
+        nc.vector.tensor_copy(ant_scales[:], scale_win[:].indirect(ant_sb[:]))
+        for o in range(PASSES):
+            nc.vector.tensor_copy(ant_words[o][:], word_win[o][:].bitcast(U32).indirect(ant_sb[:]))
+        nc.vector.tensor_copy(ant_ment[:], ment_win[:].indirect(ant_sb[:]))
+
         for b in range(BLOCKS):
             z_pass(1, b, 0)
-        gather_ant_words(0)
-        gather_ant_words(1)
-        nc.vector.tensor_copy(ant_ment[:], ment_win[:].indirect(ant_sb[:]))
-        for b in range(BLOCKS + LAG):
-            if b < BLOCKS:
-                z_pass(1, b, 1)
-                round_z(1, b)
-                quantize_z(1, b, b + 1)
-            if b >= LAG:
-                score(b - LAG)
+            z_pass(1, b, 1)
+            round_z(1, b)
+            quantize_z(1, b, b + 1)
+        for b in range(BLOCKS):
+            score(b)

@@ -36,6 +36,7 @@ def tile_picked_zcoref_sig_p_kernel(tc, x_words, x_scales, w1, ment, offs, ant, 
         keep = ctx.enter_context(tc.tile_pool(name="keep", bufs=1))
         ring = ctx.enter_context(tc.tile_pool(name="ring", bufs=BLOCKS))
         reuse = ctx.enter_context(tc.tile_pool(name="reuse", bufs=1))
+        early = ctx.enter_context(tc.tile_pool(name="early", bufs=1))
         psum = ctx.enter_context(tc.psum_pool(name="psum", bufs=BANKS))
 
         offs_sb = keep.tile([P, S // LIST_COL], U16, name="offs_sb")
@@ -44,11 +45,11 @@ def tile_picked_zcoref_sig_p_kernel(tc, x_words, x_scales, w1, ment, offs, ant, 
         word_win = [keep.tile([P, T], I32, name=f"word_win{o}", align_bytes=64) for o in range(PASSES)]
         ment_win = keep.tile([P, T], F32, name="ment_win", align_bytes=64)
 
+        nc.gpsimd.memset(scale_win[:].bitcast(I32), 0)
         warm = keep.tile([P, 2], F32, name="warm")
         nc.gpsimd.memset(warm[:, 0:1], 0.0)
         nc.scalar.activation(warm[:, 1:2], warm[:, 0:1], SIGMOID)
 
-        nc.vector.memset(scale_win[:].bitcast(I32), 0)
 
         w_raw = {}
 
@@ -60,16 +61,16 @@ def tile_picked_zcoref_sig_p_kernel(tc, x_words, x_scales, w1, ment, offs, ant, 
         def load_x(o):
             nc.sync.dma_start(word_win[o][:], x_words[o].rearrange("p n r -> p (n r)").bitcast(I32))
 
-        load_w(0, 0, 0, HALF)
         nc.sync.dma_start(offs_sb[:], offs)
+        nc.sync.dma_start(ant_sb[:], ant)
+        load_x(0)
         for q in range(QUADRANTS):
             nc.sync.dma_start(
                 scale_win[QUADRANT * q : QUADRANT * q + SCALE_ROWS * PASSES, :].bitcast(I32),
                 x_scales[:, SCALE_ROWS * q : SCALE_ROWS * (q + 1), :].bitcast(I32),
             )
-        nc.sync.dma_start(ant_sb[:], ant)
+        load_w(0, 0, 0, HALF)
         load_w(0, 0, HALF, P)
-        load_x(0)
         load_w(1, 0, 0, HALF)
         load_w(1, 0, HALF, P)
         load_x(1)
@@ -81,11 +82,12 @@ def tile_picked_zcoref_sig_p_kernel(tc, x_words, x_scales, w1, ment, offs, ant, 
         blocks = [(o, h) for h in range(PASSES) for o in range(PASSES)]
         w_codes = {(o, h): keep.tile([P, K_PASS], U32, name=f"w_codes{o}{h}", align_bytes=64) for o, h in blocks}
         w_scales = {(o, h): keep.tile([P, K_PASS], U8, name=f"w_scales{o}{h}", align_bytes=64) for o, h in blocks}
-        w_bf = {(o, h): keep.tile([P, PACK, P, PACK], BF16, name=f"w_bf{o}{h}", align_bytes=64) for o, h in blocks[:-1]}
+        w_bf = {(o, h): keep.tile([P, PACK, P, PACK], BF16, name=f"w_bf{o}{h}", align_bytes=64) for o, h in blocks[1:-1]}
+        w_bf[0, 0] = early.tile([P, PACK, P, PACK], BF16, name="w_bf00", align_bytes=64, offset=0)
         span_words = [keep.tile([P, S], U32, name=f"span_words{o}", align_bytes=64) for o in range(PASSES)]
         span_scales = keep.tile([P, S], U8, name="span_scales", align_bytes=64)
         ant_words = [keep.tile([P, V], U32, name=f"ant_words{o}", align_bytes=64) for o in range(PASSES)]
-        ant_scales = keep.tile([P, V], U8, name="ant_scales", align_bytes=64)
+        ant_scales = early.tile([P, V], U8, name="ant_scales", align_bytes=64, offset=2048)
         z_codes = [keep.tile([P, S], U32, name=f"z_codes{h}", align_bytes=64) for h in range(PASSES)]
 
         w_bf[1, 1] = reuse.tile([P, PACK, P, PACK], BF16, name="w_bf11", align_bytes=64, offset=0)
@@ -165,9 +167,9 @@ def tile_picked_zcoref_sig_p_kernel(tc, x_words, x_scales, w1, ment, offs, ant, 
             nc.scalar.activation(prob[:], logit[:], SIGMOID)
             nc.sync.dma_start(out[spans, :], prob[:])
 
+        gather_span_words(0, 0, S)
+        nc.vector.tensor_copy(ant_words[0][:], word_win[0][:].bitcast(U32).indirect(ant_sb[:]))
         nc.vector.tensor_copy(span_scales[:], scale_win[:].indirect(offs_sb[:]))
-        gather_span_words(0, 0, S // 2)
-        gather_span_words(0, S // 2, S)
         round_w(nc.scalar.copy, 0, 0, 0, 0, HALF)
         round_w(nc.scalar.copy, 0, 0, HALF, HALF, P)
         quantize_w(0, 0)
@@ -195,8 +197,7 @@ def tile_picked_zcoref_sig_p_kernel(tc, x_words, x_scales, w1, ment, offs, ant, 
                 quantize_z(0, b + 1 - Z_GROUP, b + 1)
 
         nc.vector.tensor_copy(ant_scales[:], scale_win[:].indirect(ant_sb[:]))
-        for o in range(PASSES):
-            nc.vector.tensor_copy(ant_words[o][:], word_win[o][:].bitcast(U32).indirect(ant_sb[:]))
+        nc.vector.tensor_copy(ant_words[1][:], word_win[1][:].bitcast(U32).indirect(ant_sb[:]))
         nc.vector.tensor_copy(ant_ment[:], ment_win[:].indirect(ant_sb[:]))
 
         for b in range(BLOCKS):

@@ -26,6 +26,8 @@ LIST_COL = 16
 BLOCKS = S // P
 BANKS = 8
 HALF = P // 2
+AHEAD = 7
+Z1_GROUP = 2
 VECTOR_SHARE = HALF // 2
 Z_GROUP = 4
 
@@ -73,8 +75,8 @@ def tile_picked_zcoref_sig_p_kernel(tc, x_words, x_scales, w1, ment, offs, ant, 
         load_w(0, 0, HALF, P)
         load_w(1, 0, 0, HALF)
         load_w(1, 0, HALF, P)
-        load_x(1)
         load_w(0, 1, 0, HALF)
+        load_x(1)
         load_w(0, 1, HALF, P)
         load_w(1, 1, 0, P)
         nc.sync.dma_start(ment_win[:], ment)
@@ -86,7 +88,10 @@ def tile_picked_zcoref_sig_p_kernel(tc, x_words, x_scales, w1, ment, offs, ant, 
         w_bf[0, 0] = early.tile([P, PACK, P, PACK], BF16, name="w_bf00", align_bytes=64, offset=0)
         span_words = [keep.tile([P, S], U32, name=f"span_words{o}", align_bytes=64) for o in range(PASSES)]
         span_scales = keep.tile([P, S], U8, name="span_scales", align_bytes=64)
-        ant_words = [keep.tile([P, V], U32, name=f"ant_words{o}", align_bytes=64) for o in range(PASSES)]
+        ant_words = [
+            early.tile([P, V], U32, name="ant_words0", align_bytes=64, offset=0),
+            keep.tile([P, V], U32, name="ant_words1", align_bytes=64),
+        ]
         ant_scales = early.tile([P, V], U8, name="ant_scales", align_bytes=64, offset=2048)
         z_codes = [keep.tile([P, S], U32, name=f"z_codes{h}", align_bytes=64) for h in range(PASSES)]
 
@@ -98,7 +103,7 @@ def tile_picked_zcoref_sig_p_kernel(tc, x_words, x_scales, w1, ment, offs, ant, 
         ant_ment = reuse.tile([P, V], F32, name="ant_ment", align_bytes=64, offset=S)
 
         z_bf = [
-            keep.tile([P, S, PACK], BF16, name="z_bf0", tag=f"w_raw01_{HALF}", align_bytes=64),
+            keep.tile([P, S, PACK], BF16, name="z_bf0", align_bytes=64),
             keep.tile([P, S, PACK], BF16, name="z_bf1", align_bytes=64),
         ]
         z_bank = {}
@@ -121,8 +126,8 @@ def tile_picked_zcoref_sig_p_kernel(tc, x_words, x_scales, w1, ment, offs, ant, 
                 in_=w_bf[o, h][:].rearrange("p r m j -> p (r m j)"),
             )
 
-        def z_pass(h, b, o):
-            if o == 0:
+        def z_pass(h, b, o, opens):
+            if opens:
                 z_bank[h, b] = psum.tile([P, PACK, P], F32, name="z_bank", tag="bank")
             spans = slice(b * P, (b + 1) * P)
             for r in range(PACK):
@@ -133,8 +138,8 @@ def tile_picked_zcoref_sig_p_kernel(tc, x_words, x_scales, w1, ment, offs, ant, 
                     lhsT_scale=w_scales[o, h][:, places],
                     rhs=span_words[o][:, spans].bitcast(FP8X4),
                     rhs_scale=span_scales[SCALE_ROWS * o :, spans],
-                    start=(o == 0 and r == 0),
-                    stop=(o == PASSES - 1 and r == PACK - 1),
+                    start=(opens and r == 0),
+                    stop=(not opens and r == PACK - 1),
                 )
 
         def round_z(h, b):
@@ -168,13 +173,12 @@ def tile_picked_zcoref_sig_p_kernel(tc, x_words, x_scales, w1, ment, offs, ant, 
             nc.sync.dma_start(out[spans, :], prob[:])
 
         gather_span_words(0, 0, S)
-        nc.vector.tensor_copy(ant_words[0][:], word_win[0][:].bitcast(U32).indirect(ant_sb[:]))
         nc.vector.tensor_copy(span_scales[:], scale_win[:].indirect(offs_sb[:]))
         round_w(nc.scalar.copy, 0, 0, 0, 0, HALF)
         round_w(nc.scalar.copy, 0, 0, HALF, HALF, P)
         quantize_w(0, 0)
         for b in range(BLOCKS):
-            z_pass(0, b, 0)
+            z_pass(0, b, 0, True)
 
         round_w(nc.scalar.copy, 1, 0, 0, 0, HALF)
         round_w(nc.scalar.copy, 1, 0, HALF, HALF, P)
@@ -183,27 +187,32 @@ def tile_picked_zcoref_sig_p_kernel(tc, x_words, x_scales, w1, ment, offs, ant, 
         gather_span_words(1, S // 4, S // 2)
         gather_span_words(1, S // 2, S)
 
-        round_w(nc.scalar.copy, 0, 1, 0, 0, HALF - VECTOR_SHARE)
-        round_w(nc.scalar.copy, 0, 1, HALF, HALF, P)
-        round_w(nc.vector.tensor_copy, 0, 1, 0, HALF - VECTOR_SHARE, HALF)
+        round_w(nc.scalar.copy, 0, 1, 0, 0, HALF)
+        round_w(nc.scalar.copy, 0, 1, HALF, HALF, P - VECTOR_SHARE)
+        round_w(nc.vector.tensor_copy, 0, 1, HALF, P - VECTOR_SHARE, P)
         quantize_w(0, 1)
         round_w(nc.vector.tensor_copy, 1, 1, 0, 0, P)
         quantize_w(1, 1)
 
         for b in range(BLOCKS):
-            z_pass(0, b, 1)
+            z_pass(0, b, 1, False)
             round_z(0, b)
             if (b + 1) % Z_GROUP == 0:
                 quantize_z(0, b + 1 - Z_GROUP, b + 1)
 
         nc.vector.tensor_copy(ant_scales[:], scale_win[:].indirect(ant_sb[:]))
-        nc.vector.tensor_copy(ant_words[1][:], word_win[1][:].bitcast(U32).indirect(ant_sb[:]))
+        for o in range(PASSES):
+            nc.vector.tensor_copy(ant_words[o][:], word_win[o][:].bitcast(U32).indirect(ant_sb[:]))
         nc.vector.tensor_copy(ant_ment[:], ment_win[:].indirect(ant_sb[:]))
 
+        for b in range(AHEAD):
+            z_pass(1, b, 0, True)
         for b in range(BLOCKS):
-            z_pass(1, b, 0)
-            z_pass(1, b, 1)
+            z_pass(1, b, 1, b >= AHEAD)
+            if b >= AHEAD:
+                z_pass(1, b, 0, False)
             round_z(1, b)
-            quantize_z(1, b, b + 1)
+            if (b + 1) % Z1_GROUP == 0:
+                quantize_z(1, b + 1 - Z1_GROUP, b + 1)
         for b in range(BLOCKS):
             score(b)

@@ -28,8 +28,7 @@ BANKS = 8
 HALF = P // 2
 AHEAD = 7
 Z1_GROUP = 2
-VECTOR_SHARE = HALF // 2
-Z_GROUP = 4
+Z_GROUP = 8
 
 
 def tile_picked_zcoref_sig_p_kernel(tc, x_words, x_scales, w1, ment, offs, ant, out):
@@ -38,7 +37,6 @@ def tile_picked_zcoref_sig_p_kernel(tc, x_words, x_scales, w1, ment, offs, ant, 
         keep = ctx.enter_context(tc.tile_pool(name="keep", bufs=1))
         ring = ctx.enter_context(tc.tile_pool(name="ring", bufs=BLOCKS))
         reuse = ctx.enter_context(tc.tile_pool(name="reuse", bufs=1))
-        early = ctx.enter_context(tc.tile_pool(name="early", bufs=1))
         psum = ctx.enter_context(tc.psum_pool(name="psum", bufs=BANKS))
 
         offs_sb = keep.tile([P, S // LIST_COL], U16, name="offs_sb")
@@ -47,16 +45,21 @@ def tile_picked_zcoref_sig_p_kernel(tc, x_words, x_scales, w1, ment, offs, ant, 
         word_win = [keep.tile([P, T], I32, name=f"word_win{o}", align_bytes=64) for o in range(PASSES)]
         ment_win = keep.tile([P, T], F32, name="ment_win", align_bytes=64)
 
-        nc.gpsimd.memset(scale_win[:].bitcast(I32), 0)
         warm = keep.tile([P, 2], F32, name="warm")
         nc.gpsimd.memset(warm[:, 0:1], 0.0)
         nc.scalar.activation(warm[:, 1:2], warm[:, 0:1], SIGMOID)
 
+        nc.vector.memset(scale_win[:].bitcast(I32), 0)
 
         w_raw = {}
+        shared = {(1, 1, 0): reuse}
 
         def load_w(o, h, first, last):
-            w_raw[o, h, first] = keep.tile([P, PACK, PACK * (last - first)], F32, name=f"w_raw{o}{h}_{first}", align_bytes=64)
+            shape = [P, PACK, PACK * (last - first)]
+            if (o, h, first) in shared:
+                w_raw[o, h, first] = shared[o, h, first].tile(shape, F32, name=f"w_raw{o}{h}_{first}", align_bytes=64, offset=0)
+            else:
+                w_raw[o, h, first] = keep.tile(shape, F32, name=f"w_raw{o}{h}_{first}", align_bytes=64)
             rows = w1[o * K_PASS : (o + 1) * K_PASS, h * K_PASS + PACK * first : h * K_PASS + PACK * last]
             nc.sync.dma_start(w_raw[o, h, first][:], rows.rearrange("(p j) c -> p j c", j=PACK))
 
@@ -65,7 +68,6 @@ def tile_picked_zcoref_sig_p_kernel(tc, x_words, x_scales, w1, ment, offs, ant, 
 
         nc.sync.dma_start(offs_sb[:], offs)
         nc.sync.dma_start(ant_sb[:], ant)
-        load_x(0)
         for q in range(QUADRANTS):
             nc.sync.dma_start(
                 scale_win[QUADRANT * q : QUADRANT * q + SCALE_ROWS * PASSES, :].bitcast(I32),
@@ -73,10 +75,11 @@ def tile_picked_zcoref_sig_p_kernel(tc, x_words, x_scales, w1, ment, offs, ant, 
             )
         load_w(0, 0, 0, HALF)
         load_w(0, 0, HALF, P)
+        load_x(0)
         load_w(1, 0, 0, HALF)
         load_w(1, 0, HALF, P)
-        load_w(0, 1, 0, HALF)
         load_x(1)
+        load_w(0, 1, 0, HALF)
         load_w(0, 1, HALF, P)
         load_w(1, 1, 0, P)
         nc.sync.dma_start(ment_win[:], ment)
@@ -84,18 +87,13 @@ def tile_picked_zcoref_sig_p_kernel(tc, x_words, x_scales, w1, ment, offs, ant, 
         blocks = [(o, h) for h in range(PASSES) for o in range(PASSES)]
         w_codes = {(o, h): keep.tile([P, K_PASS], U32, name=f"w_codes{o}{h}", align_bytes=64) for o, h in blocks}
         w_scales = {(o, h): keep.tile([P, K_PASS], U8, name=f"w_scales{o}{h}", align_bytes=64) for o, h in blocks}
-        w_bf = {(o, h): keep.tile([P, PACK, P, PACK], BF16, name=f"w_bf{o}{h}", align_bytes=64) for o, h in blocks[1:-1]}
-        w_bf[0, 0] = early.tile([P, PACK, P, PACK], BF16, name="w_bf00", align_bytes=64, offset=0)
+        w_bf = {(o, h): keep.tile([P, PACK, P, PACK], BF16, name=f"w_bf{o}{h}", align_bytes=64) for o, h in blocks}
         span_words = [keep.tile([P, S], U32, name=f"span_words{o}", align_bytes=64) for o in range(PASSES)]
         span_scales = keep.tile([P, S], U8, name="span_scales", align_bytes=64)
-        ant_words = [
-            early.tile([P, V], U32, name="ant_words0", align_bytes=64, offset=0),
-            keep.tile([P, V], U32, name="ant_words1", align_bytes=64),
-        ]
-        ant_scales = early.tile([P, V], U8, name="ant_scales", align_bytes=64, offset=2048)
+        ant_words = [keep.tile([P, V], U32, name=f"ant_words{o}", align_bytes=64) for o in range(PASSES)]
+        ant_scales = keep.tile([P, V], U8, name="ant_scales", align_bytes=64)
         z_codes = [keep.tile([P, S], U32, name=f"z_codes{h}", align_bytes=64) for h in range(PASSES)]
 
-        w_bf[1, 1] = reuse.tile([P, PACK, P, PACK], BF16, name="w_bf11", align_bytes=64, offset=0)
         z_scales = [
             reuse.tile([P, S], U8, name="z_scales0", align_bytes=64, offset=0),
             keep.tile([P, S], U8, name="z_scales1", align_bytes=64),
@@ -172,11 +170,13 @@ def tile_picked_zcoref_sig_p_kernel(tc, x_words, x_scales, w1, ment, offs, ant, 
             nc.scalar.activation(prob[:], logit[:], SIGMOID)
             nc.sync.dma_start(out[spans, :], prob[:])
 
-        gather_span_words(0, 0, S)
         nc.vector.tensor_copy(span_scales[:], scale_win[:].indirect(offs_sb[:]))
+        nc.vector.tensor_copy(ant_scales[:], scale_win[:].indirect(ant_sb[:]))
         round_w(nc.scalar.copy, 0, 0, 0, 0, HALF)
         round_w(nc.scalar.copy, 0, 0, HALF, HALF, P)
         quantize_w(0, 0)
+        gather_span_words(0, 0, S // 2)
+        gather_span_words(0, S // 2, S)
         for b in range(BLOCKS):
             z_pass(0, b, 0, True)
 
@@ -184,12 +184,10 @@ def tile_picked_zcoref_sig_p_kernel(tc, x_words, x_scales, w1, ment, offs, ant, 
         round_w(nc.scalar.copy, 1, 0, HALF, HALF, P)
         quantize_w(1, 0)
         gather_span_words(1, 0, S // 4)
-        gather_span_words(1, S // 4, S // 2)
-        gather_span_words(1, S // 2, S)
+        gather_span_words(1, S // 4, S)
 
         round_w(nc.scalar.copy, 0, 1, 0, 0, HALF)
-        round_w(nc.scalar.copy, 0, 1, HALF, HALF, P - VECTOR_SHARE)
-        round_w(nc.vector.tensor_copy, 0, 1, HALF, P - VECTOR_SHARE, P)
+        round_w(nc.vector.tensor_copy, 0, 1, HALF, HALF, P)
         quantize_w(0, 1)
         round_w(nc.vector.tensor_copy, 1, 1, 0, 0, P)
         quantize_w(1, 1)
@@ -200,7 +198,6 @@ def tile_picked_zcoref_sig_p_kernel(tc, x_words, x_scales, w1, ment, offs, ant, 
             if (b + 1) % Z_GROUP == 0:
                 quantize_z(0, b + 1 - Z_GROUP, b + 1)
 
-        nc.vector.tensor_copy(ant_scales[:], scale_win[:].indirect(ant_sb[:]))
         for o in range(PASSES):
             nc.vector.tensor_copy(ant_words[o][:], word_win[o][:].bitcast(U32).indirect(ant_sb[:]))
         nc.vector.tensor_copy(ant_ment[:], ment_win[:].indirect(ant_sb[:]))

@@ -25,6 +25,7 @@ SCALE_ROWS = 4
 LIST_COL = 16
 BLOCKS = S // P
 BANKS = 8
+CUT = 64
 HALF = P // 2
 AHEAD = 7
 Z1_GROUP = 2
@@ -37,6 +38,7 @@ def tile_picked_zcoref_sig_p_kernel(tc, x_words, x_scales, w1, ment, offs, ant, 
         keep = ctx.enter_context(tc.tile_pool(name="keep", bufs=1))
         ring = ctx.enter_context(tc.tile_pool(name="ring", bufs=BLOCKS))
         reuse = ctx.enter_context(tc.tile_pool(name="reuse", bufs=1))
+        reuse01 = ctx.enter_context(tc.tile_pool(name="reuse01", bufs=1))
         psum = ctx.enter_context(tc.psum_pool(name="psum", bufs=BANKS))
 
         offs_sb = keep.tile([P, S // LIST_COL], U16, name="offs_sb")
@@ -52,7 +54,7 @@ def tile_picked_zcoref_sig_p_kernel(tc, x_words, x_scales, w1, ment, offs, ant, 
         nc.vector.memset(scale_win[:].bitcast(I32), 0)
 
         w_raw = {}
-        shared = {(1, 1, 0): reuse}
+        shared = {(1, 1, 0): reuse, (0, 1, 0): reuse01}
 
         def load_w(o, h, first, last):
             shape = [P, PACK, PACK * (last - first)]
@@ -79,8 +81,8 @@ def tile_picked_zcoref_sig_p_kernel(tc, x_words, x_scales, w1, ment, offs, ant, 
         load_w(1, 0, 0, HALF)
         load_w(1, 0, HALF, P)
         load_x(1)
-        load_w(0, 1, 0, HALF)
-        load_w(0, 1, HALF, P)
+        load_w(0, 1, 0, CUT)
+        load_w(0, 1, CUT, P)
         load_w(1, 1, 0, P)
         nc.sync.dma_start(ment_win[:], ment)
 
@@ -90,7 +92,10 @@ def tile_picked_zcoref_sig_p_kernel(tc, x_words, x_scales, w1, ment, offs, ant, 
         w_bf = {(o, h): keep.tile([P, PACK, P, PACK], BF16, name=f"w_bf{o}{h}", align_bytes=64) for o, h in blocks}
         span_words = [keep.tile([P, S], U32, name=f"span_words{o}", align_bytes=64) for o in range(PASSES)]
         span_scales = keep.tile([P, S], U8, name="span_scales", align_bytes=64)
-        ant_words = [keep.tile([P, V], U32, name=f"ant_words{o}", align_bytes=64) for o in range(PASSES)]
+        ant_words = [
+            keep.tile([P, V], U32, name="ant_words0", align_bytes=64),
+            reuse01.tile([P, V], U32, name="ant_words1", align_bytes=64, offset=0),
+        ]
         ant_scales = keep.tile([P, V], U8, name="ant_scales", align_bytes=64)
         z_codes = [keep.tile([P, S], U32, name=f"z_codes{h}", align_bytes=64) for h in range(PASSES)]
 
@@ -101,7 +106,7 @@ def tile_picked_zcoref_sig_p_kernel(tc, x_words, x_scales, w1, ment, offs, ant, 
         ant_ment = reuse.tile([P, V], F32, name="ant_ment", align_bytes=64, offset=S)
 
         z_bf = [
-            keep.tile([P, S, PACK], BF16, name="z_bf0", align_bytes=64),
+            reuse01.tile([P, S, PACK], BF16, name="z_bf0", align_bytes=64, offset=4 * V),
             keep.tile([P, S, PACK], BF16, name="z_bf1", align_bytes=64),
         ]
         z_bank = {}
@@ -110,6 +115,9 @@ def tile_picked_zcoref_sig_p_kernel(tc, x_words, x_scales, w1, ment, offs, ant, 
             entries = offs_sb[:, first // LIST_COL : last // LIST_COL]
             nc.vector.tensor_copy(span_words[o][:, first:last], word_win[o][:].bitcast(U32).indirect(entries))
 
+        def gather_ant_words(o):
+            nc.vector.tensor_copy(ant_words[o][:], word_win[o][:].bitcast(U32).indirect(ant_sb[:]))
+
         def round_w(copy, o, h, piece, first, last):
             cols = slice(PACK * (first - piece), PACK * (last - piece))
             copy(
@@ -117,11 +125,18 @@ def tile_picked_zcoref_sig_p_kernel(tc, x_words, x_scales, w1, ment, offs, ant, 
                 w_raw[o, h, piece][:, :, cols].rearrange("p j (m r) -> p m j r", r=PACK),
             )
 
-        def quantize_w(o, h):
+        def round_places(copy, o, h, first, last):
+            copy(
+                w_bf[o, h][:, first:last, :, :].rearrange("p r m j -> p m j r"),
+                w_raw[o, h, 0][:].rearrange("p j (m r) -> p m j r", r=PACK)[:, :, :, first:last],
+            )
+
+        def quantize_w(o, h, first=0, last=PACK):
+            places = slice(first * P, last * P)
             nc.vector.quantize_mx(
-                out=w_codes[o, h][:].bitcast(FP8X4),
-                scales=w_scales[o, h][:],
-                in_=w_bf[o, h][:].rearrange("p r m j -> p (r m j)"),
+                out=w_codes[o, h][:, places].bitcast(FP8X4),
+                scales=w_scales[o, h][:, places],
+                in_=w_bf[o, h][:, first:last].rearrange("p r m j -> p (r m j)"),
             )
 
         def z_pass(h, b, o, opens):
@@ -186,11 +201,14 @@ def tile_picked_zcoref_sig_p_kernel(tc, x_words, x_scales, w1, ment, offs, ant, 
         gather_span_words(1, 0, S // 4)
         gather_span_words(1, S // 4, S)
 
-        round_w(nc.scalar.copy, 0, 1, 0, 0, HALF)
-        round_w(nc.vector.tensor_copy, 0, 1, HALF, HALF, P)
+        round_w(nc.scalar.copy, 0, 1, 0, 0, CUT)
+        round_w(nc.vector.tensor_copy, 0, 1, CUT, CUT, P)
+        gather_ant_words(1)
         quantize_w(0, 1)
-        round_w(nc.vector.tensor_copy, 1, 1, 0, 0, P)
-        quantize_w(1, 1)
+        round_places(nc.vector.tensor_copy, 1, 1, 0, 2)
+        round_places(nc.vector.tensor_copy, 1, 1, 2, 4)
+        quantize_w(1, 1, 0, 2)
+        quantize_w(1, 1, 2, 4)
 
         for b in range(BLOCKS):
             z_pass(0, b, 1, False)
@@ -198,8 +216,7 @@ def tile_picked_zcoref_sig_p_kernel(tc, x_words, x_scales, w1, ment, offs, ant, 
             if (b + 1) % Z_GROUP == 0:
                 quantize_z(0, b + 1 - Z_GROUP, b + 1)
 
-        for o in range(PASSES):
-            nc.vector.tensor_copy(ant_words[o][:], word_win[o][:].bitcast(U32).indirect(ant_sb[:]))
+        gather_ant_words(0)
         nc.vector.tensor_copy(ant_ment[:], ment_win[:].indirect(ant_sb[:]))
 
         for b in range(AHEAD):

@@ -13,6 +13,7 @@ U16 = mybir.dt.uint16
 U8 = mybir.dt.uint8
 FP8X4 = mybir.dt.float8_e4m3fn_x4
 SIGMOID = mybir.ActivationFunctionType.Sigmoid
+COPY = mybir.ActivationFunctionType.Copy
 ADD = mybir.AluOpType.add
 
 P = 128
@@ -29,6 +30,10 @@ CUT = 64
 HALF = P // 2
 AHEAD = 7
 Z1_GROUP = 2
+MENT_ROW = 16
+SPREAD = 8
+X_FIRST = 512
+LATE = 3 * S // 4
 Z_GROUP = 8
 
 
@@ -36,7 +41,6 @@ def tile_picked_zcoref_sig_p_kernel(tc, x_words, x_scales, w1, ment, offs, ant, 
     nc = tc.nc
     with ExitStack() as ctx:
         keep = ctx.enter_context(tc.tile_pool(name="keep", bufs=1))
-        ring = ctx.enter_context(tc.tile_pool(name="ring", bufs=BLOCKS))
         reuse = ctx.enter_context(tc.tile_pool(name="reuse", bufs=1))
         reuse01 = ctx.enter_context(tc.tile_pool(name="reuse01", bufs=1))
         psum = ctx.enter_context(tc.psum_pool(name="psum", bufs=BANKS))
@@ -52,6 +56,7 @@ def tile_picked_zcoref_sig_p_kernel(tc, x_words, x_scales, w1, ment, offs, ant, 
         nc.scalar.activation(warm[:, 1:2], warm[:, 0:1], SIGMOID)
 
         nc.vector.memset(scale_win[:].bitcast(I32), 0)
+        nc.vector.memset(ment_win[:].bitcast(I32), 0)
 
         w_raw = {}
         shared = {(1, 1, 0): reuse, (0, 1, 0): reuse01}
@@ -65,11 +70,13 @@ def tile_picked_zcoref_sig_p_kernel(tc, x_words, x_scales, w1, ment, offs, ant, 
             rows = w1[o * K_PASS : (o + 1) * K_PASS, h * K_PASS + PACK * first : h * K_PASS + PACK * last]
             nc.sync.dma_start(w_raw[o, h, first][:], rows.rearrange("(p j) c -> p j c", j=PACK))
 
-        def load_x(o):
-            nc.sync.dma_start(word_win[o][:], x_words[o].rearrange("p n r -> p (n r)").bitcast(I32))
+        def load_x(o, first=0, last=T):
+            words = x_words[o].rearrange("p n r -> p (n r)").bitcast(I32)
+            nc.sync.dma_start(word_win[o][:, first:last], words[:, first:last])
 
         nc.sync.dma_start(offs_sb[:], offs)
         nc.sync.dma_start(ant_sb[:], ant)
+        load_x(0, 0, X_FIRST)
         for q in range(QUADRANTS):
             nc.sync.dma_start(
                 scale_win[QUADRANT * q : QUADRANT * q + SCALE_ROWS * PASSES, :].bitcast(I32),
@@ -77,14 +84,14 @@ def tile_picked_zcoref_sig_p_kernel(tc, x_words, x_scales, w1, ment, offs, ant, 
             )
         load_w(0, 0, 0, HALF)
         load_w(0, 0, HALF, P)
-        load_x(0)
+        nc.sync.dma_start(ment_win[MENT_ROW : MENT_ROW + 1, :], ment[0:1, :])
+        load_x(0, X_FIRST, T)
         load_w(1, 0, 0, HALF)
         load_w(1, 0, HALF, P)
         load_x(1)
         load_w(0, 1, 0, CUT)
         load_w(0, 1, CUT, P)
         load_w(1, 1, 0, P)
-        nc.sync.dma_start(ment_win[:], ment)
 
         blocks = [(o, h) for h in range(PASSES) for o in range(PASSES)]
         w_codes = {(o, h): keep.tile([P, K_PASS], U32, name=f"w_codes{o}{h}", align_bytes=64) for o, h in blocks}
@@ -92,9 +99,10 @@ def tile_picked_zcoref_sig_p_kernel(tc, x_words, x_scales, w1, ment, offs, ant, 
         w_bf = {(o, h): keep.tile([P, PACK, P, PACK], BF16, name=f"w_bf{o}{h}", align_bytes=64) for o, h in blocks}
         span_words = [keep.tile([P, S], U32, name=f"span_words{o}", align_bytes=64) for o in range(PASSES)]
         span_scales = keep.tile([P, S], U8, name="span_scales", align_bytes=64)
+        late_words = reuse01.tile([P, S - LATE], U32, name="late_words", align_bytes=64, offset=0)
         ant_words = [
             keep.tile([P, V], U32, name="ant_words0", align_bytes=64),
-            reuse01.tile([P, V], U32, name="ant_words1", align_bytes=64, offset=0),
+            reuse.tile([P, V], U32, name="ant_words1", align_bytes=64, offset=S),
         ]
         ant_scales = keep.tile([P, V], U8, name="ant_scales", align_bytes=64)
         z_codes = [keep.tile([P, S], U32, name=f"z_codes{h}", align_bytes=64) for h in range(PASSES)]
@@ -103,17 +111,25 @@ def tile_picked_zcoref_sig_p_kernel(tc, x_words, x_scales, w1, ment, offs, ant, 
             reuse.tile([P, S], U8, name="z_scales0", align_bytes=64, offset=0),
             keep.tile([P, S], U8, name="z_scales1", align_bytes=64),
         ]
-        ant_ment = reuse.tile([P, V], F32, name="ant_ment", align_bytes=64, offset=S)
+        ant_ment = keep.tile([P, V], F32, name="ant_ment", align_bytes=64)
+        ment_row = keep.tile([P, V], F32, name="ment_row", align_bytes=64)
+        ment_few = keep.tile([P, V], F32, name="ment_few", align_bytes=64)
 
         z_bf = [
             reuse01.tile([P, S, PACK], BF16, name="z_bf0", align_bytes=64, offset=4 * V),
             keep.tile([P, S, PACK], BF16, name="z_bf1", align_bytes=64),
         ]
         z_bank = {}
+        logit = [keep.tile([P, V], F32, name=f"logit{b}", align_bytes=64) for b in range(BLOCKS)]
+        prob = [keep.tile([P, V], F32, name=f"prob{b}", align_bytes=64) for b in range(BLOCKS)]
 
         def gather_span_words(o, first, last):
             entries = offs_sb[:, first // LIST_COL : last // LIST_COL]
             nc.vector.tensor_copy(span_words[o][:, first:last], word_win[o][:].bitcast(U32).indirect(entries))
+
+        def gather_late_words():
+            entries = offs_sb[:, LATE // LIST_COL :]
+            nc.vector.tensor_copy(late_words[:], word_win[1][:].bitcast(U32).indirect(entries))
 
         def gather_ant_words(o):
             nc.vector.tensor_copy(ant_words[o][:], word_win[o][:].bitcast(U32).indirect(ant_sb[:]))
@@ -143,20 +159,23 @@ def tile_picked_zcoref_sig_p_kernel(tc, x_words, x_scales, w1, ment, offs, ant, 
             if opens:
                 z_bank[h, b] = psum.tile([P, PACK, P], F32, name="z_bank", tag="bank")
             spans = slice(b * P, (b + 1) * P)
+            words = span_words[o][:, spans]
+            if o == 1 and b * P >= LATE:
+                words = late_words[:, b * P - LATE : (b + 1) * P - LATE]
             for r in range(PACK):
                 places = slice(r * P, (r + 1) * P)
                 nc.tensor.matmul_mx(
                     out=z_bank[h, b][:, r, :],
                     lhsT=w_codes[o, h][:, places].bitcast(FP8X4),
                     lhsT_scale=w_scales[o, h][:, places],
-                    rhs=span_words[o][:, spans].bitcast(FP8X4),
+                    rhs=words.bitcast(FP8X4),
                     rhs_scale=span_scales[SCALE_ROWS * o :, spans],
                     start=(opens and r == 0),
                     stop=(not opens and r == PACK - 1),
                 )
 
-        def round_z(h, b):
-            nc.scalar.copy(z_bf[h][:, b * P : (b + 1) * P, :], z_bank[h, b][:].rearrange("p r n -> p n r"))
+        def round_z(h, b, copy=nc.scalar.copy):
+            copy(z_bf[h][:, b * P : (b + 1) * P, :], z_bank[h, b][:].rearrange("p r n -> p n r"))
 
         def quantize_z(h, first, last):
             spans = slice(first * P, last * P)
@@ -165,6 +184,11 @@ def tile_picked_zcoref_sig_p_kernel(tc, x_words, x_scales, w1, ment, offs, ant, 
                 scales=z_scales[h][:, spans],
                 in_=z_bf[h][:, spans, :].rearrange("p n r -> p (n r)"),
             )
+
+        def pieces(b):
+            if b < BLOCKS - 1:
+                return [slice(0, V)]
+            return [slice(0, V // 2), slice(V // 2, V)]
 
         def score(b):
             spans = slice(b * P, (b + 1) * P)
@@ -179,16 +203,22 @@ def tile_picked_zcoref_sig_p_kernel(tc, x_words, x_scales, w1, ment, offs, ant, 
                     start=(h == 0),
                     stop=(h == PASSES - 1),
                 )
-            logit = ring.tile([P, V], F32, name="logit")
-            nc.vector.tensor_tensor(logit[:], y_bank[:], ant_ment[:], ADD)
-            prob = ring.tile([P, V], F32, name="prob")
-            nc.scalar.activation(prob[:], logit[:], SIGMOID)
-            nc.sync.dma_start(out[spans, :], prob[:])
+            for cols in pieces(b):
+                nc.vector.tensor_tensor(logit[b][:, cols], y_bank[:, cols], ant_ment[:, cols], ADD)
+
+        def finish(b):
+            for cols in pieces(b):
+                nc.scalar.activation(prob[b][:, cols], logit[b][:, cols], SIGMOID)
+            nc.sync.dma_start(out[b * P : (b + 1) * P, :], prob[b][:])
 
         nc.vector.tensor_copy(span_scales[:], scale_win[:].indirect(offs_sb[:]))
         nc.vector.tensor_copy(ant_scales[:], scale_win[:].indirect(ant_sb[:]))
         round_w(nc.scalar.copy, 0, 0, 0, 0, HALF)
         round_w(nc.scalar.copy, 0, 0, HALF, HALF, P)
+        nc.scalar.activation(ment_row[:], ment_win[:].indirect(ant_sb[:]), COPY)
+        few = ment_few[0 : PACK * SPREAD : PACK, :]
+        nc.sync.dma_start(few, ment_row[MENT_ROW : MENT_ROW + 1, :].unsqueeze(1).to_broadcast([1, SPREAD, V]))
+        nc.sync.dma_start(ant_ment[:], few.unsqueeze(1).to_broadcast([SPREAD, P // SPREAD, V]))
         quantize_w(0, 0)
         gather_span_words(0, 0, S // 2)
         gather_span_words(0, S // 2, S)
@@ -199,16 +229,17 @@ def tile_picked_zcoref_sig_p_kernel(tc, x_words, x_scales, w1, ment, offs, ant, 
         round_w(nc.scalar.copy, 1, 0, HALF, HALF, P)
         quantize_w(1, 0)
         gather_span_words(1, 0, S // 4)
-        gather_span_words(1, S // 4, S)
+        gather_span_words(1, S // 4, LATE)
 
         round_w(nc.scalar.copy, 0, 1, 0, 0, CUT)
         round_w(nc.vector.tensor_copy, 0, 1, CUT, CUT, P)
-        gather_ant_words(1)
+        gather_late_words()
         quantize_w(0, 1)
         round_places(nc.vector.tensor_copy, 1, 1, 0, 2)
         round_places(nc.vector.tensor_copy, 1, 1, 2, 4)
         quantize_w(1, 1, 0, 2)
         quantize_w(1, 1, 2, 4)
+        gather_ant_words(1)
 
         for b in range(BLOCKS):
             z_pass(0, b, 1, False)
@@ -217,16 +248,34 @@ def tile_picked_zcoref_sig_p_kernel(tc, x_words, x_scales, w1, ment, offs, ant, 
                 quantize_z(0, b + 1 - Z_GROUP, b + 1)
 
         gather_ant_words(0)
-        nc.vector.tensor_copy(ant_ment[:], ment_win[:].indirect(ant_sb[:]))
 
         for b in range(AHEAD):
             z_pass(1, b, 0, True)
-        for b in range(BLOCKS):
+        def close_z(b):
             z_pass(1, b, 1, b >= AHEAD)
             if b >= AHEAD:
                 z_pass(1, b, 0, False)
-            round_z(1, b)
-            if (b + 1) % Z1_GROUP == 0:
-                quantize_z(1, b + 1 - Z1_GROUP, b + 1)
+
         for b in range(BLOCKS):
+            close_z(b)
+        round_z(1, 0)
+        round_z(1, 1)
+        quantize_z(1, 0, 2)
+        round_z(1, 7, nc.vector.tensor_copy)
+        round_z(1, 2)
+        round_z(1, 3)
+        quantize_z(1, 2, 4)
+        round_z(1, 4)
+        round_z(1, 5)
+        round_z(1, 6)
+        score(0)
+        score(1)
+        quantize_z(1, 4, 6)
+        score(2)
+        quantize_z(1, 6, 8)
+        finish(0)
+        finish(1)
+        finish(2)
+        for b in range(3, BLOCKS):
             score(b)
+            finish(b)

@@ -28,7 +28,7 @@ BLOCKS = S // P
 BANKS = 8
 CUT = 64
 HALF = P // 2
-AHEAD = 7
+AHEAD = 6
 Z1_GROUP = 2
 MENT_ROW = 16
 SPREAD = 8
@@ -120,6 +120,7 @@ def tile_picked_zcoref_sig_p_kernel(tc, x_words, x_scales, w1, ment, offs, ant, 
             keep.tile([P, S, PACK], BF16, name="z_bf1", align_bytes=64),
         ]
         z_bank = {}
+        y_bank = {}
         logit = [keep.tile([P, V], F32, name=f"logit{b}", align_bytes=64) for b in range(BLOCKS)]
         prob = [keep.tile([P, V], F32, name=f"prob{b}", align_bytes=64) for b in range(BLOCKS)]
 
@@ -191,11 +192,15 @@ def tile_picked_zcoref_sig_p_kernel(tc, x_words, x_scales, w1, ment, offs, ant, 
             return [slice(0, V // 2), slice(V // 2, V)]
 
         def score(b):
+            score_mm(b)
+            add_ment(b)
+
+        def score_mm(b):
             spans = slice(b * P, (b + 1) * P)
-            y_bank = psum.tile([P, V], F32, name="y_bank", tag="bank")
+            y_bank[b] = psum.tile([P, V], F32, name="y_bank", tag="bank")
             for h in range(PASSES):
                 nc.tensor.matmul_mx(
-                    out=y_bank[:],
+                    out=y_bank[b][:],
                     lhsT=z_codes[h][:, spans].bitcast(FP8X4),
                     lhsT_scale=z_scales[h][:, spans],
                     rhs=ant_words[h][:].bitcast(FP8X4),
@@ -203,8 +208,10 @@ def tile_picked_zcoref_sig_p_kernel(tc, x_words, x_scales, w1, ment, offs, ant, 
                     start=(h == 0),
                     stop=(h == PASSES - 1),
                 )
+
+        def add_ment(b):
             for cols in pieces(b):
-                nc.vector.tensor_tensor(logit[b][:, cols], y_bank[:, cols], ant_ment[:, cols], ADD)
+                nc.vector.tensor_tensor(logit[b][:, cols], y_bank[b][:, cols], ant_ment[:, cols], ADD)
 
         def finish(b):
             for cols in pieces(b):
@@ -256,21 +263,23 @@ def tile_picked_zcoref_sig_p_kernel(tc, x_words, x_scales, w1, ment, offs, ant, 
             if b >= AHEAD:
                 z_pass(1, b, 0, False)
 
-        for b in range(BLOCKS):
+        for b in range(BLOCKS - 1):
             close_z(b)
         round_z(1, 0)
         round_z(1, 1)
         quantize_z(1, 0, 2)
-        round_z(1, 7, nc.vector.tensor_copy)
+        round_z(1, 5, nc.vector.tensor_copy)
         round_z(1, 2)
         round_z(1, 3)
         quantize_z(1, 2, 4)
         round_z(1, 4)
-        round_z(1, 5)
         round_z(1, 6)
-        score(0)
-        score(1)
+        score_mm(0)
+        close_z(7)
+        round_z(1, 7)
+        add_ment(0)
         quantize_z(1, 4, 6)
+        score(1)
         score(2)
         quantize_z(1, 6, 8)
         finish(0)

@@ -27,6 +27,7 @@ LIST_COL = 16
 BLOCKS = S // P
 BANKS = 8
 CUT = 64
+LAST_CUT = 64
 HALF = P // 2
 AHEAD = 6
 Z1_GROUP = 2
@@ -59,7 +60,7 @@ def tile_picked_zcoref_sig_p_kernel(tc, x_words, x_scales, w1, ment, offs, ant, 
         nc.vector.memset(ment_win[:].bitcast(I32), 0)
 
         w_raw = {}
-        shared = {(1, 1, 0): reuse, (0, 1, 0): reuse01}
+        shared = {(1, 1, LAST_CUT): reuse, (0, 1, 0): reuse01}
 
         def load_w(o, h, first, last):
             shape = [P, PACK, PACK * (last - first)]
@@ -91,7 +92,8 @@ def tile_picked_zcoref_sig_p_kernel(tc, x_words, x_scales, w1, ment, offs, ant, 
         load_x(1)
         load_w(0, 1, 0, CUT)
         load_w(0, 1, CUT, P)
-        load_w(1, 1, 0, P)
+        load_w(1, 1, 0, LAST_CUT)
+        load_w(1, 1, LAST_CUT, P)
 
         blocks = [(o, h) for h in range(PASSES) for o in range(PASSES)]
         w_codes = {(o, h): keep.tile([P, K_PASS], U32, name=f"w_codes{o}{h}", align_bytes=64) for o, h in blocks}
@@ -142,10 +144,10 @@ def tile_picked_zcoref_sig_p_kernel(tc, x_words, x_scales, w1, ment, offs, ant, 
                 w_raw[o, h, piece][:, :, cols].rearrange("p j (m r) -> p m j r", r=PACK),
             )
 
-        def round_places(copy, o, h, first, last):
+        def round_places(copy, o, h, piece, first, last):
             copy(
-                w_bf[o, h][:, first:last, :, :].rearrange("p r m j -> p m j r"),
-                w_raw[o, h, 0][:].rearrange("p j (m r) -> p m j r", r=PACK)[:, :, :, first:last],
+                w_bf[o, h][:, first:last, piece:, :].rearrange("p r m j -> p m j r"),
+                w_raw[o, h, piece][:].rearrange("p j (m r) -> p m j r", r=PACK)[:, :, :, first:last],
             )
 
         def quantize_w(o, h, first=0, last=PACK):
@@ -197,21 +199,23 @@ def tile_picked_zcoref_sig_p_kernel(tc, x_words, x_scales, w1, ment, offs, ant, 
 
         def score_mm(b):
             spans = slice(b * P, (b + 1) * P)
-            y_bank[b] = psum.tile([P, V], F32, name="y_bank", tag="bank")
-            for h in range(PASSES):
-                nc.tensor.matmul_mx(
-                    out=y_bank[b][:],
-                    lhsT=z_codes[h][:, spans].bitcast(FP8X4),
-                    lhsT_scale=z_scales[h][:, spans],
-                    rhs=ant_words[h][:].bitcast(FP8X4),
-                    rhs_scale=ant_scales[SCALE_ROWS * h :, :],
-                    start=(h == 0),
-                    stop=(h == PASSES - 1),
-                )
+            for cols in pieces(b):
+                width = cols.stop - cols.start
+                y_bank[b, cols.start] = psum.tile([P, width], F32, name="y_bank", tag="bank")
+                for h in range(PASSES):
+                    nc.tensor.matmul_mx(
+                        out=y_bank[b, cols.start][:],
+                        lhsT=z_codes[h][:, spans].bitcast(FP8X4),
+                        lhsT_scale=z_scales[h][:, spans],
+                        rhs=ant_words[h][:, cols].bitcast(FP8X4),
+                        rhs_scale=ant_scales[SCALE_ROWS * h :, cols],
+                        start=(h == 0),
+                        stop=(h == PASSES - 1),
+                    )
 
         def add_ment(b):
             for cols in pieces(b):
-                nc.vector.tensor_tensor(logit[b][:, cols], y_bank[b][:, cols], ant_ment[:, cols], ADD)
+                nc.vector.tensor_tensor(logit[b][:, cols], y_bank[b, cols.start][:], ant_ment[:, cols], ADD)
 
         def finish(b):
             for cols in pieces(b):
@@ -235,15 +239,17 @@ def tile_picked_zcoref_sig_p_kernel(tc, x_words, x_scales, w1, ment, offs, ant, 
         round_w(nc.scalar.copy, 1, 0, 0, 0, HALF)
         round_w(nc.scalar.copy, 1, 0, HALF, HALF, P)
         quantize_w(1, 0)
-        gather_span_words(1, 0, S // 4)
-        gather_span_words(1, S // 4, LATE)
+        gather_span_words(1, 0, P)
+        gather_span_words(1, P, 3 * P)
+        gather_span_words(1, 3 * P, LATE)
 
         round_w(nc.scalar.copy, 0, 1, 0, 0, CUT)
         round_w(nc.vector.tensor_copy, 0, 1, CUT, CUT, P)
         gather_late_words()
         quantize_w(0, 1)
-        round_places(nc.vector.tensor_copy, 1, 1, 0, 2)
-        round_places(nc.vector.tensor_copy, 1, 1, 2, 4)
+        round_w(nc.vector.tensor_copy, 1, 1, 0, 0, LAST_CUT)
+        round_places(nc.vector.tensor_copy, 1, 1, LAST_CUT, 0, 2)
+        round_places(nc.vector.tensor_copy, 1, 1, LAST_CUT, 2, 4)
         quantize_w(1, 1, 0, 2)
         quantize_w(1, 1, 2, 4)
         gather_ant_words(1)
@@ -268,23 +274,25 @@ def tile_picked_zcoref_sig_p_kernel(tc, x_words, x_scales, w1, ment, offs, ant, 
         round_z(1, 0)
         round_z(1, 1)
         quantize_z(1, 0, 2)
-        round_z(1, 5, nc.vector.tensor_copy)
         round_z(1, 2)
         round_z(1, 3)
         quantize_z(1, 2, 4)
         round_z(1, 4)
+        round_z(1, 5)
         round_z(1, 6)
         score_mm(0)
         close_z(7)
         round_z(1, 7)
         add_ment(0)
-        quantize_z(1, 4, 6)
         score(1)
+        quantize_z(1, 4, 6)
         score(2)
+        score(3)
         quantize_z(1, 6, 8)
         finish(0)
         finish(1)
         finish(2)
-        for b in range(3, BLOCKS):
+        finish(3)
+        for b in range(4, BLOCKS):
             score(b)
             finish(b)

@@ -18,6 +18,7 @@ ADD = mybir.AluOpType.add
 
 P = 128
 PACK = 4
+WORD_BYTES = 4
 K_PASS = P * PACK
 PASSES = K // K_PASS
 QUADRANTS = 4
@@ -25,25 +26,23 @@ QUADRANT = P // QUADRANTS
 SCALE_ROWS = 4
 LIST_COL = 16
 BLOCKS = S // P
+LAST = BLOCKS - 1
 BANKS = 8
-CUT = 64
-LAST_CUT = 64
 HALF = P // 2
+QUARTER = P // 4
+X_FIRST = T // 4
+LATE = 3 * S // 4
 AHEAD = 6
-Z1_GROUP = 2
 MENT_ROW = 16
 SPREAD = 8
-X_FIRST = 512
-LATE = 3 * S // 4
-Z_GROUP = 8
 
 
 def tile_picked_zcoref_sig_p_kernel(tc, x_words, x_scales, w1, ment, offs, ant, out):
     nc = tc.nc
     with ExitStack() as ctx:
         keep = ctx.enter_context(tc.tile_pool(name="keep", bufs=1))
-        reuse = ctx.enter_context(tc.tile_pool(name="reuse", bufs=1))
-        reuse01 = ctx.enter_context(tc.tile_pool(name="reuse01", bufs=1))
+        after11 = ctx.enter_context(tc.tile_pool(name="after11", bufs=1))
+        after01 = ctx.enter_context(tc.tile_pool(name="after01", bufs=1))
         psum = ctx.enter_context(tc.psum_pool(name="psum", bufs=BANKS))
 
         offs_sb = keep.tile([P, S // LIST_COL], U16, name="offs_sb")
@@ -60,18 +59,19 @@ def tile_picked_zcoref_sig_p_kernel(tc, x_words, x_scales, w1, ment, offs, ant, 
         nc.vector.memset(ment_win[:].bitcast(I32), 0)
 
         w_raw = {}
-        shared = {(1, 1, LAST_CUT): reuse, (0, 1, 0): reuse01}
+        shared = {(1, 1, HALF): after11, (0, 1, QUARTER): after01}
 
         def load_w(o, h, first, last):
             shape = [P, PACK, PACK * (last - first)]
+            name = f"w_raw{o}{h}_{first}"
             if (o, h, first) in shared:
-                w_raw[o, h, first] = shared[o, h, first].tile(shape, F32, name=f"w_raw{o}{h}_{first}", align_bytes=64, offset=0)
+                w_raw[o, h, first] = shared[o, h, first].tile(shape, F32, name=name, align_bytes=64, offset=0)
             else:
-                w_raw[o, h, first] = keep.tile(shape, F32, name=f"w_raw{o}{h}_{first}", align_bytes=64)
+                w_raw[o, h, first] = keep.tile(shape, F32, name=name, align_bytes=64)
             rows = w1[o * K_PASS : (o + 1) * K_PASS, h * K_PASS + PACK * first : h * K_PASS + PACK * last]
             nc.sync.dma_start(w_raw[o, h, first][:], rows.rearrange("(p j) c -> p j c", j=PACK))
 
-        def load_x(o, first=0, last=T):
+        def load_x(o, first, last):
             words = x_words[o].rearrange("p n r -> p (n r)").bitcast(I32)
             nc.sync.dma_start(word_win[o][:, first:last], words[:, first:last])
 
@@ -89,36 +89,36 @@ def tile_picked_zcoref_sig_p_kernel(tc, x_words, x_scales, w1, ment, offs, ant, 
         load_x(0, X_FIRST, T)
         load_w(1, 0, 0, HALF)
         load_w(1, 0, HALF, P)
-        load_x(1)
-        load_w(0, 1, 0, CUT)
-        load_w(0, 1, CUT, P)
-        load_w(1, 1, 0, LAST_CUT)
-        load_w(1, 1, LAST_CUT, P)
+        load_x(1, 0, T)
+        load_w(0, 1, 0, QUARTER)
+        load_w(0, 1, QUARTER, HALF)
+        load_w(0, 1, HALF, P)
+        load_w(1, 1, 0, HALF)
+        load_w(1, 1, HALF, P)
 
-        blocks = [(o, h) for h in range(PASSES) for o in range(PASSES)]
-        w_codes = {(o, h): keep.tile([P, K_PASS], U32, name=f"w_codes{o}{h}", align_bytes=64) for o, h in blocks}
-        w_scales = {(o, h): keep.tile([P, K_PASS], U8, name=f"w_scales{o}{h}", align_bytes=64) for o, h in blocks}
-        w_bf = {(o, h): keep.tile([P, PACK, P, PACK], BF16, name=f"w_bf{o}{h}", align_bytes=64) for o, h in blocks}
+        squares = [(o, h) for h in range(PASSES) for o in range(PASSES)]
+        w_codes = {(o, h): keep.tile([P, K_PASS], U32, name=f"w_codes{o}{h}", align_bytes=64) for o, h in squares}
+        w_scales = {(o, h): keep.tile([P, K_PASS], U8, name=f"w_scales{o}{h}", align_bytes=64) for o, h in squares}
+        w_bf = {(o, h): keep.tile([P, PACK, P, PACK], BF16, name=f"w_bf{o}{h}", align_bytes=64) for o, h in squares}
         span_words = [keep.tile([P, S], U32, name=f"span_words{o}", align_bytes=64) for o in range(PASSES)]
         span_scales = keep.tile([P, S], U8, name="span_scales", align_bytes=64)
-        late_words = reuse01.tile([P, S - LATE], U32, name="late_words", align_bytes=64, offset=0)
+
+        late_words = after01.tile([P, S - LATE], U32, name="late_words", align_bytes=64, offset=0)
         ant_words = [
             keep.tile([P, V], U32, name="ant_words0", align_bytes=64),
-            reuse.tile([P, V], U32, name="ant_words1", align_bytes=64, offset=S),
+            after11.tile([P, V], U32, name="ant_words1", align_bytes=64, offset=S),
         ]
         ant_scales = keep.tile([P, V], U8, name="ant_scales", align_bytes=64)
         z_codes = [keep.tile([P, S], U32, name=f"z_codes{h}", align_bytes=64) for h in range(PASSES)]
-
         z_scales = [
-            reuse.tile([P, S], U8, name="z_scales0", align_bytes=64, offset=0),
+            after11.tile([P, S], U8, name="z_scales0", align_bytes=64, offset=0),
             keep.tile([P, S], U8, name="z_scales1", align_bytes=64),
         ]
         ant_ment = keep.tile([P, V], F32, name="ant_ment", align_bytes=64)
         ment_row = keep.tile([P, V], F32, name="ment_row", align_bytes=64)
         ment_few = keep.tile([P, V], F32, name="ment_few", align_bytes=64)
-
         z_bf = [
-            reuse01.tile([P, S, PACK], BF16, name="z_bf0", align_bytes=64, offset=4 * V),
+            after01.tile([P, S, PACK], BF16, name="z_bf0", align_bytes=64, offset=WORD_BYTES * (S - LATE)),
             keep.tile([P, S, PACK], BF16, name="z_bf1", align_bytes=64),
         ]
         z_bank = {}
@@ -137,25 +137,18 @@ def tile_picked_zcoref_sig_p_kernel(tc, x_words, x_scales, w1, ment, offs, ant, 
         def gather_ant_words(o):
             nc.vector.tensor_copy(ant_words[o][:], word_win[o][:].bitcast(U32).indirect(ant_sb[:]))
 
-        def round_w(copy, o, h, piece, first, last):
-            cols = slice(PACK * (first - piece), PACK * (last - piece))
+        def round_w(copy, o, h, first, last, r_first=0, r_last=PACK):
             copy(
-                w_bf[o, h][:, :, first:last, :].rearrange("p r m j -> p m j r"),
-                w_raw[o, h, piece][:, :, cols].rearrange("p j (m r) -> p m j r", r=PACK),
+                w_bf[o, h][:, r_first:r_last, first:last, :].rearrange("p r m j -> p m j r"),
+                w_raw[o, h, first][:].rearrange("p j (m r) -> p m j r", r=PACK)[:, :, :, r_first:r_last],
             )
 
-        def round_places(copy, o, h, piece, first, last):
-            copy(
-                w_bf[o, h][:, first:last, piece:, :].rearrange("p r m j -> p m j r"),
-                w_raw[o, h, piece][:].rearrange("p j (m r) -> p m j r", r=PACK)[:, :, :, first:last],
-            )
-
-        def quantize_w(o, h, first=0, last=PACK):
-            places = slice(first * P, last * P)
+        def quantize_w(o, h, r_first=0, r_last=PACK):
+            places = slice(r_first * P, r_last * P)
             nc.vector.quantize_mx(
                 out=w_codes[o, h][:, places].bitcast(FP8X4),
                 scales=w_scales[o, h][:, places],
-                in_=w_bf[o, h][:, first:last].rearrange("p r m j -> p (r m j)"),
+                in_=w_bf[o, h][:, r_first:r_last].rearrange("p r m j -> p (r m j)"),
             )
 
         def z_pass(h, b, o, opens):
@@ -177,8 +170,13 @@ def tile_picked_zcoref_sig_p_kernel(tc, x_words, x_scales, w1, ment, offs, ant, 
                     stop=(not opens and r == PACK - 1),
                 )
 
-        def round_z(h, b, copy=nc.scalar.copy):
-            copy(z_bf[h][:, b * P : (b + 1) * P, :], z_bank[h, b][:].rearrange("p r n -> p n r"))
+        def close_second_half(b):
+            z_pass(1, b, 1, b >= AHEAD)
+            if b >= AHEAD:
+                z_pass(1, b, 0, False)
+
+        def round_z(h, b):
+            nc.scalar.copy(z_bf[h][:, b * P : (b + 1) * P, :], z_bank[h, b][:].rearrange("p r n -> p n r"))
 
         def quantize_z(h, first, last):
             spans = slice(first * P, last * P)
@@ -188,20 +186,15 @@ def tile_picked_zcoref_sig_p_kernel(tc, x_words, x_scales, w1, ment, offs, ant, 
                 in_=z_bf[h][:, spans, :].rearrange("p n r -> p (n r)"),
             )
 
-        def pieces(b):
-            if b < BLOCKS - 1:
+        def column_runs(b):
+            if b < LAST:
                 return [slice(0, V)]
             return [slice(0, V // 2), slice(V // 2, V)]
 
-        def score(b):
-            score_mm(b)
-            add_ment(b)
-
-        def score_mm(b):
+        def score_product(b):
             spans = slice(b * P, (b + 1) * P)
-            for cols in pieces(b):
-                width = cols.stop - cols.start
-                y_bank[b, cols.start] = psum.tile([P, width], F32, name="y_bank", tag="bank")
+            for cols in column_runs(b):
+                y_bank[b, cols.start] = psum.tile([P, cols.stop - cols.start], F32, name="y_bank", tag="bank")
                 for h in range(PASSES):
                     nc.tensor.matmul_mx(
                         out=y_bank[b, cols.start][:],
@@ -214,85 +207,81 @@ def tile_picked_zcoref_sig_p_kernel(tc, x_words, x_scales, w1, ment, offs, ant, 
                     )
 
         def add_ment(b):
-            for cols in pieces(b):
+            for cols in column_runs(b):
                 nc.vector.tensor_tensor(logit[b][:, cols], y_bank[b, cols.start][:], ant_ment[:, cols], ADD)
 
+        def score(b):
+            score_product(b)
+            add_ment(b)
+
         def finish(b):
-            for cols in pieces(b):
+            for cols in column_runs(b):
                 nc.scalar.activation(prob[b][:, cols], logit[b][:, cols], SIGMOID)
             nc.sync.dma_start(out[b * P : (b + 1) * P, :], prob[b][:])
 
         nc.vector.tensor_copy(span_scales[:], scale_win[:].indirect(offs_sb[:]))
         nc.vector.tensor_copy(ant_scales[:], scale_win[:].indirect(ant_sb[:]))
-        round_w(nc.scalar.copy, 0, 0, 0, 0, HALF)
-        round_w(nc.scalar.copy, 0, 0, HALF, HALF, P)
+        round_w(nc.scalar.copy, 0, 0, 0, HALF)
+        round_w(nc.scalar.copy, 0, 0, HALF, P)
+
         nc.scalar.activation(ment_row[:], ment_win[:].indirect(ant_sb[:]), COPY)
         few = ment_few[0 : PACK * SPREAD : PACK, :]
         nc.sync.dma_start(few, ment_row[MENT_ROW : MENT_ROW + 1, :].unsqueeze(1).to_broadcast([1, SPREAD, V]))
         nc.sync.dma_start(ant_ment[:], few.unsqueeze(1).to_broadcast([SPREAD, P // SPREAD, V]))
+
         quantize_w(0, 0)
         gather_span_words(0, 0, S // 2)
         gather_span_words(0, S // 2, S)
         for b in range(BLOCKS):
             z_pass(0, b, 0, True)
 
-        round_w(nc.scalar.copy, 1, 0, 0, 0, HALF)
-        round_w(nc.scalar.copy, 1, 0, HALF, HALF, P)
+        round_w(nc.scalar.copy, 1, 0, 0, HALF)
+        round_w(nc.scalar.copy, 1, 0, HALF, P)
         quantize_w(1, 0)
         gather_span_words(1, 0, P)
         gather_span_words(1, P, 3 * P)
         gather_span_words(1, 3 * P, LATE)
 
-        round_w(nc.scalar.copy, 0, 1, 0, 0, CUT)
-        round_w(nc.vector.tensor_copy, 0, 1, CUT, CUT, P)
+        round_w(nc.scalar.copy, 0, 1, 0, QUARTER)
+        round_w(nc.scalar.copy, 0, 1, QUARTER, HALF)
+        round_w(nc.vector.tensor_copy, 0, 1, HALF, P)
         gather_late_words()
         quantize_w(0, 1)
-        round_w(nc.vector.tensor_copy, 1, 1, 0, 0, LAST_CUT)
-        round_places(nc.vector.tensor_copy, 1, 1, LAST_CUT, 0, 2)
-        round_places(nc.vector.tensor_copy, 1, 1, LAST_CUT, 2, 4)
-        quantize_w(1, 1, 0, 2)
-        quantize_w(1, 1, 2, 4)
+        round_w(nc.vector.tensor_copy, 1, 1, 0, HALF)
+        round_w(nc.vector.tensor_copy, 1, 1, HALF, P, 0, PACK // 2)
+        round_w(nc.vector.tensor_copy, 1, 1, HALF, P, PACK // 2, PACK)
+        quantize_w(1, 1, 0, PACK // 2)
+        quantize_w(1, 1, PACK // 2, PACK)
         gather_ant_words(1)
 
         for b in range(BLOCKS):
             z_pass(0, b, 1, False)
             round_z(0, b)
-            if (b + 1) % Z_GROUP == 0:
-                quantize_z(0, b + 1 - Z_GROUP, b + 1)
+        quantize_z(0, 0, BLOCKS)
 
         gather_ant_words(0)
 
         for b in range(AHEAD):
             z_pass(1, b, 0, True)
-        def close_z(b):
-            z_pass(1, b, 1, b >= AHEAD)
-            if b >= AHEAD:
-                z_pass(1, b, 0, False)
-
-        for b in range(BLOCKS - 1):
-            close_z(b)
-        round_z(1, 0)
-        round_z(1, 1)
-        quantize_z(1, 0, 2)
-        round_z(1, 2)
-        round_z(1, 3)
-        quantize_z(1, 2, 4)
-        round_z(1, 4)
-        round_z(1, 5)
-        round_z(1, 6)
-        score_mm(0)
-        close_z(7)
-        round_z(1, 7)
+        for b in range(LAST):
+            close_second_half(b)
+        for first in (0, 2):
+            round_z(1, first)
+            round_z(1, first + 1)
+            quantize_z(1, first, first + 2)
+        for b in range(4, LAST):
+            round_z(1, b)
+        score_product(0)
+        close_second_half(LAST)
+        round_z(1, LAST)
         add_ment(0)
         score(1)
         quantize_z(1, 4, 6)
         score(2)
         score(3)
         quantize_z(1, 6, 8)
-        finish(0)
-        finish(1)
-        finish(2)
-        finish(3)
+        for b in range(4):
+            finish(b)
         for b in range(4, BLOCKS):
             score(b)
             finish(b)

@@ -244,7 +244,8 @@ def tile_picked_zcoref_sig_p_kernel(tc, x_words, x_scales, w1, ment, offs, ant, 
 
         round_w(nc.scalar.copy, 0, 1, 0, QUARTER)
         round_w(nc.scalar.copy, 0, 1, QUARTER, HALF)
-        round_w(nc.vector.tensor_copy, 0, 1, HALF, P)
+        round_w(nc.scalar.copy, 0, 1, HALF, P, 0, PACK // 2)
+        round_w(nc.vector.tensor_copy, 0, 1, HALF, P, PACK // 2, PACK)
         gather_late_words()
         quantize_w(0, 1)
         round_w(nc.vector.tensor_copy, 1, 1, 0, HALF)

@@ -33,6 +33,7 @@ QUARTER = P // 4
 X_FIRST = T // 4
 LATE = 3 * S // 4
 AHEAD = 6
+FIRST_AHEAD = 6
 MENT_ROW = 16
 SPREAD = 8
 
@@ -232,7 +233,7 @@ def tile_picked_zcoref_sig_p_kernel(tc, x_words, x_scales, w1, ment, offs, ant, 
         quantize_w(0, 0)
         gather_span_words(0, 0, S // 2)
         gather_span_words(0, S // 2, S)
-        for b in range(BLOCKS):
+        for b in range(FIRST_AHEAD):
             z_pass(0, b, 0, True)
 
         round_w(nc.scalar.copy, 1, 0, 0, HALF)
@@ -256,7 +257,9 @@ def tile_picked_zcoref_sig_p_kernel(tc, x_words, x_scales, w1, ment, offs, ant, 
         gather_ant_words(1)
 
         for b in range(BLOCKS):
-            z_pass(0, b, 1, False)
+            z_pass(0, b, 1, b >= FIRST_AHEAD)
+            if b >= FIRST_AHEAD:
+                z_pass(0, b, 0, False)
             round_z(0, b)
         quantize_z(0, 0, BLOCKS)
 

@@ -18,108 +18,108 @@ ADD = mybir.AluOpType.add
 
 P = 128
 PACK = 4
-WORD_BYTES = 4
 K_PASS = P * PACK
 PASSES = K // K_PASS
 QUADRANTS = 4
 QUADRANT = P // QUADRANTS
 SCALE_ROWS = 4
+PASS_ROWS = QUADRANTS * SCALE_ROWS
 LIST_COL = 16
 BLOCKS = S // P
 LAST = BLOCKS - 1
 BANKS = 8
 HALF = P // 2
-QUARTER = P // 4
-X_FIRST = T // 4
-LATE = 3 * S // 4
+HALF_BYTES = PACK * PACK * HALF * 4
 AHEAD = 6
 FIRST_AHEAD = 6
-MENT_ROW = 16
+ROWS_AT = P - PASSES * PASS_ROWS
+MENT_ROW = P - 1
 SPREAD = 8
+LATE = S - P
 
 
 def tile_picked_zcoref_sig_p_kernel(tc, x_words, x_scales, w1, ment, offs, ant, out):
     nc = tc.nc
     with ExitStack() as ctx:
         keep = ctx.enter_context(tc.tile_pool(name="keep", bufs=1))
-        after11 = ctx.enter_context(tc.tile_pool(name="after11", bufs=1))
-        after01 = ctx.enter_context(tc.tile_pool(name="after01", bufs=1))
+        buf_a = ctx.enter_context(tc.tile_pool(name="buf_a", bufs=1))
+        buf_b = ctx.enter_context(tc.tile_pool(name="buf_b", bufs=1))
+        buf_c = ctx.enter_context(tc.tile_pool(name="buf_c", bufs=1))
+        buf_d = ctx.enter_context(tc.tile_pool(name="buf_d", bufs=1))
+        buf_e = ctx.enter_context(tc.tile_pool(name="buf_e", bufs=1))
+        buf_f = ctx.enter_context(tc.tile_pool(name="buf_f", bufs=1))
+        buf_g = ctx.enter_context(tc.tile_pool(name="buf_g", bufs=1))
+        buf_h = ctx.enter_context(tc.tile_pool(name="buf_h", bufs=1))
         psum = ctx.enter_context(tc.psum_pool(name="psum", bufs=BANKS))
 
         offs_sb = keep.tile([P, S // LIST_COL], U16, name="offs_sb")
         ant_sb = keep.tile([P, V // LIST_COL], U16, name="ant_sb")
-        scale_win = keep.tile([P, T], U8, name="scale_win", align_bytes=64)
-        word_win = [keep.tile([P, T], I32, name=f"word_win{o}", align_bytes=64) for o in range(PASSES)]
-        ment_win = keep.tile([P, T], F32, name="ment_win", align_bytes=64)
+        scale_win = buf_a.tile([P, T], U8, name="scale_win", align_bytes=64, offset=0)
+        word_win = [
+            keep.tile([P, T], I32, name="word_win0", align_bytes=64),
+            buf_a.tile([P, T], I32, name="word_win1", align_bytes=64, offset=0),
+        ]
+        ment_win = buf_c.tile([P, T], F32, name="ment_win", align_bytes=64, offset=0)
 
         warm = keep.tile([P, 2], F32, name="warm")
         nc.gpsimd.memset(warm[:, 0:1], 0.0)
         nc.scalar.activation(warm[:, 1:2], warm[:, 0:1], SIGMOID)
 
-        nc.vector.memset(scale_win[:].bitcast(I32), 0)
-        nc.vector.memset(ment_win[:].bitcast(I32), 0)
+        nc.vector.memset(scale_win[0:ROWS_AT, :].bitcast(I32), 0)
+        nc.vector.memset(ment_win[0:MENT_ROW, :].bitcast(I32), 0)
 
         w_raw = {}
-        shared = {(1, 1, HALF): after11, (0, 1, QUARTER): after01}
+        places = {
+            (0, 0, 0): (buf_h, 0),
+            (0, 0, HALF): (buf_b, HALF_BYTES),
+            (1, 0, 0): (buf_d, 0),
+            (1, 0, HALF): (buf_f, 0),
+            (0, 1, 0): (buf_h, 0),
+            (0, 1, HALF): (buf_b, HALF_BYTES),
+            (1, 1, 0): (buf_d, 0),
+            (1, 1, HALF): (buf_f, 0),
+        }
 
         def load_w(o, h, first, last):
-            shape = [P, PACK, PACK * (last - first)]
-            name = f"w_raw{o}{h}_{first}"
-            if (o, h, first) in shared:
-                w_raw[o, h, first] = shared[o, h, first].tile(shape, F32, name=name, align_bytes=64, offset=0)
-            else:
-                w_raw[o, h, first] = keep.tile(shape, F32, name=name, align_bytes=64)
+            pool, offset = places[o, h, first]
+            w_raw[o, h, first] = pool.tile(
+                [P, PACK, PACK * (last - first)], F32, name=f"w_raw{o}{h}_{first}", align_bytes=64, offset=offset
+            )
             rows = w1[o * K_PASS : (o + 1) * K_PASS, h * K_PASS + PACK * first : h * K_PASS + PACK * last]
             nc.sync.dma_start(w_raw[o, h, first][:], rows.rearrange("(p j) c -> p j c", j=PACK))
 
-        def load_x(o, first, last):
-            words = x_words[o].rearrange("p n r -> p (n r)").bitcast(I32)
-            nc.sync.dma_start(word_win[o][:, first:last], words[:, first:last])
-
-        nc.sync.dma_start(offs_sb[:], offs)
-        nc.sync.dma_start(ant_sb[:], ant)
-        load_x(0, 0, X_FIRST)
-        for q in range(QUADRANTS):
-            nc.sync.dma_start(
-                scale_win[QUADRANT * q : QUADRANT * q + SCALE_ROWS * PASSES, :].bitcast(I32),
-                x_scales[:, SCALE_ROWS * q : SCALE_ROWS * (q + 1), :].bitcast(I32),
-            )
-        load_w(0, 0, 0, HALF)
-        load_w(0, 0, HALF, P)
-        nc.sync.dma_start(ment_win[MENT_ROW : MENT_ROW + 1, :], ment[0:1, :])
-        load_x(0, X_FIRST, T)
-        load_w(1, 0, 0, HALF)
-        load_w(1, 0, HALF, P)
-        load_x(1, 0, T)
-        load_w(0, 1, 0, QUARTER)
-        load_w(0, 1, QUARTER, HALF)
-        load_w(0, 1, HALF, P)
-        load_w(1, 1, 0, HALF)
-        load_w(1, 1, HALF, P)
+        def load_x(o):
+            nc.sync.dma_start(word_win[o][:], x_words[o].rearrange("p n r -> p (n r)").bitcast(I32))
 
         squares = [(o, h) for h in range(PASSES) for o in range(PASSES)]
         w_codes = {(o, h): keep.tile([P, K_PASS], U32, name=f"w_codes{o}{h}", align_bytes=64) for o, h in squares}
         w_scales = {(o, h): keep.tile([P, K_PASS], U8, name=f"w_scales{o}{h}", align_bytes=64) for o, h in squares}
-        w_bf = {(o, h): keep.tile([P, PACK, P, PACK], BF16, name=f"w_bf{o}{h}", align_bytes=64) for o, h in squares}
+        w_bf = {
+            (o, h): keep.tile([P, PACK, P, PACK], BF16, name=f"w_bf{o}{h}", align_bytes=64)
+            for o, h in squares
+            if h == 1
+        }
+        w_bf[0, 0] = buf_g.tile([P, PACK, P, PACK], BF16, name="w_bf00", align_bytes=64, offset=0)
+        w_bf[1, 0] = buf_e.tile([P, PACK, P, PACK], BF16, name="w_bf10", align_bytes=64, offset=0)
         span_words = [keep.tile([P, S], U32, name=f"span_words{o}", align_bytes=64) for o in range(PASSES)]
+        span_rows = keep.tile([P, S], U8, name="span_rows", align_bytes=64)
+        ant_rows = keep.tile([P, V], U8, name="ant_rows", align_bytes=64)
         span_scales = keep.tile([P, S], U8, name="span_scales", align_bytes=64)
-
-        late_words = after01.tile([P, S - LATE], U32, name="late_words", align_bytes=64, offset=0)
-        ant_words = [
-            keep.tile([P, V], U32, name="ant_words0", align_bytes=64),
-            after11.tile([P, V], U32, name="ant_words1", align_bytes=64, offset=S),
-        ]
-        ant_scales = keep.tile([P, V], U8, name="ant_scales", align_bytes=64)
+        ant_scales = buf_e.tile([P, V], U8, name="ant_scales", align_bytes=64, offset=4 * V)
+        ant_words0 = buf_g.tile([P, V], U32, name="ant_words0", align_bytes=64, offset=0)
+        ant_words1 = buf_f.tile([P, V], U32, name="ant_words1", align_bytes=64, offset=S)
+        ant_words = [ant_words0, ant_words1]
+        late_words = buf_b.tile([P, S - LATE], U32, name="late_words", align_bytes=64, offset=HALF_BYTES)
         z_codes = [keep.tile([P, S], U32, name=f"z_codes{h}", align_bytes=64) for h in range(PASSES)]
         z_scales = [
-            after11.tile([P, S], U8, name="z_scales0", align_bytes=64, offset=0),
+            buf_f.tile([P, S], U8, name="z_scales0", align_bytes=64, offset=0),
             keep.tile([P, S], U8, name="z_scales1", align_bytes=64),
         ]
         ant_ment = keep.tile([P, V], F32, name="ant_ment", align_bytes=64)
         ment_row = keep.tile([P, V], F32, name="ment_row", align_bytes=64)
-        ment_few = keep.tile([P, V], F32, name="ment_few", align_bytes=64)
+        ment_few = buf_e.tile([P, V], F32, name="ment_few", align_bytes=64, offset=0)
         z_bf = [
-            after01.tile([P, S, PACK], BF16, name="z_bf0", align_bytes=64, offset=WORD_BYTES * (S - LATE)),
+            buf_h.tile([P, S, PACK], BF16, name="z_bf0", align_bytes=64, offset=0),
             keep.tile([P, S, PACK], BF16, name="z_bf1", align_bytes=64),
         ]
         z_bank = {}
@@ -127,28 +127,33 @@ def tile_picked_zcoref_sig_p_kernel(tc, x_words, x_scales, w1, ment, offs, ant, 
         logit = [keep.tile([P, V], F32, name=f"logit{b}", align_bytes=64) for b in range(BLOCKS)]
         prob = [keep.tile([P, V], F32, name=f"prob{b}", align_bytes=64) for b in range(BLOCKS)]
 
+        def place_rows(scales, rows):
+            for q in range(QUADRANTS):
+                nc.sync.dma_start(
+                    scales[QUADRANT * q : QUADRANT * q + PASSES * SCALE_ROWS, :].bitcast(I32),
+                    rows[ROWS_AT + q : P : QUADRANTS, :].bitcast(I32),
+                )
+
         def gather_span_words(o, first, last):
             entries = offs_sb[:, first // LIST_COL : last // LIST_COL]
             nc.vector.tensor_copy(span_words[o][:, first:last], word_win[o][:].bitcast(U32).indirect(entries))
 
-        def gather_late_words():
-            entries = offs_sb[:, LATE // LIST_COL :]
-            nc.vector.tensor_copy(late_words[:], word_win[1][:].bitcast(U32).indirect(entries))
+        def gather_ant_words(into, o, first, last):
+            entries = ant_sb[:, first // LIST_COL : last // LIST_COL]
+            nc.vector.tensor_copy(into[:], word_win[o][:].bitcast(U32).indirect(entries))
 
-        def gather_ant_words(o):
-            nc.vector.tensor_copy(ant_words[o][:], word_win[o][:].bitcast(U32).indirect(ant_sb[:]))
-
-        def round_w(copy, o, h, first, last, r_first=0, r_last=PACK):
+        def round_w(copy, o, h, piece, first, last, r_first=0, r_last=PACK):
+            raw = w_raw[o, h, piece][:].rearrange("p j (m r) -> p m j r", r=PACK)
             copy(
                 w_bf[o, h][:, r_first:r_last, first:last, :].rearrange("p r m j -> p m j r"),
-                w_raw[o, h, first][:].rearrange("p j (m r) -> p m j r", r=PACK)[:, :, :, r_first:r_last],
+                raw[:, first - piece : last - piece, :, r_first:r_last],
             )
 
         def quantize_w(o, h, r_first=0, r_last=PACK):
-            places = slice(r_first * P, r_last * P)
+            cols = slice(r_first * P, r_last * P)
             nc.vector.quantize_mx(
-                out=w_codes[o, h][:, places].bitcast(FP8X4),
-                scales=w_scales[o, h][:, places],
+                out=w_codes[o, h][:, cols].bitcast(FP8X4),
+                scales=w_scales[o, h][:, cols],
                 in_=w_bf[o, h][:, r_first:r_last].rearrange("p r m j -> p (r m j)"),
             )
 
@@ -160,11 +165,11 @@ def tile_picked_zcoref_sig_p_kernel(tc, x_words, x_scales, w1, ment, offs, ant, 
             if o == 1 and b * P >= LATE:
                 words = late_words[:, b * P - LATE : (b + 1) * P - LATE]
             for r in range(PACK):
-                places = slice(r * P, (r + 1) * P)
+                cols = slice(r * P, (r + 1) * P)
                 nc.tensor.matmul_mx(
                     out=z_bank[h, b][:, r, :],
-                    lhsT=w_codes[o, h][:, places].bitcast(FP8X4),
-                    lhsT_scale=w_scales[o, h][:, places],
+                    lhsT=w_codes[o, h][:, cols].bitcast(FP8X4),
+                    lhsT_scale=w_scales[o, h][:, cols],
                     rhs=words.bitcast(FP8X4),
                     rhs_scale=span_scales[SCALE_ROWS * o :, spans],
                     start=(opens and r == 0),
@@ -192,20 +197,24 @@ def tile_picked_zcoref_sig_p_kernel(tc, x_words, x_scales, w1, ment, offs, ant, 
                 return [slice(0, V)]
             return [slice(0, V // 2), slice(V // 2, V)]
 
-        def score_product(b):
+        def score_pass(b, bank, h, words, cols, start, stop):
             spans = slice(b * P, (b + 1) * P)
+            nc.tensor.matmul_mx(
+                out=bank,
+                lhsT=z_codes[h][:, spans].bitcast(FP8X4),
+                lhsT_scale=z_scales[h][:, spans],
+                rhs=words.bitcast(FP8X4),
+                rhs_scale=ant_scales[SCALE_ROWS * h :, cols],
+                start=start,
+                stop=stop,
+            )
+
+        def score_product(b):
             for cols in column_runs(b):
-                y_bank[b, cols.start] = psum.tile([P, cols.stop - cols.start], F32, name="y_bank", tag="bank")
+                bank = psum.tile([P, cols.stop - cols.start], F32, name="y_bank", tag="bank")
+                y_bank[b, cols.start] = bank
                 for h in range(PASSES):
-                    nc.tensor.matmul_mx(
-                        out=y_bank[b, cols.start][:],
-                        lhsT=z_codes[h][:, spans].bitcast(FP8X4),
-                        lhsT_scale=z_scales[h][:, spans],
-                        rhs=ant_words[h][:, cols].bitcast(FP8X4),
-                        rhs_scale=ant_scales[SCALE_ROWS * h :, cols],
-                        start=(h == 0),
-                        stop=(h == PASSES - 1),
-                    )
+                    score_pass(b, bank[:], h, ant_words[h][:, cols], cols, h == 0, h == PASSES - 1)
 
         def add_ment(b):
             for cols in column_runs(b):
@@ -220,41 +229,60 @@ def tile_picked_zcoref_sig_p_kernel(tc, x_words, x_scales, w1, ment, offs, ant, 
                 nc.scalar.activation(prob[b][:, cols], logit[b][:, cols], SIGMOID)
             nc.sync.dma_start(out[b * P : (b + 1) * P, :], prob[b][:])
 
-        nc.vector.tensor_copy(span_scales[:], scale_win[:].indirect(offs_sb[:]))
-        nc.vector.tensor_copy(ant_scales[:], scale_win[:].indirect(ant_sb[:]))
-        round_w(nc.scalar.copy, 0, 0, 0, HALF)
-        round_w(nc.scalar.copy, 0, 0, HALF, P)
+        for o in range(PASSES):
+            nc.sync.dma_start(
+                scale_win[ROWS_AT + PASS_ROWS * o : ROWS_AT + PASS_ROWS * (o + 1), :].bitcast(I32),
+                x_scales[o].bitcast(I32).rearrange("(q r) c -> r q c", r=SCALE_ROWS),
+            )
+        nc.sync.dma_start(offs_sb[:], offs)
+        nc.sync.dma_start(ant_sb[:], ant)
+        load_x(0)
+        nc.sync.dma_start(ment_win[MENT_ROW : MENT_ROW + 1, :], ment[0:1, :])
+        load_w(0, 0, 0, HALF)
+        load_w(0, 0, HALF, P)
+        load_w(1, 0, 0, HALF)
+        load_w(1, 0, HALF, P)
+
+        nc.vector.tensor_copy(span_rows[:], scale_win[:].indirect(offs_sb[:]))
+        place_rows(span_scales, span_rows)
+        nc.vector.tensor_copy(ant_rows[:], scale_win[:].indirect(ant_sb[:]))
+        load_x(1)
 
         nc.scalar.activation(ment_row[:], ment_win[:].indirect(ant_sb[:]), COPY)
-        few = ment_few[0 : PACK * SPREAD : PACK, :]
-        nc.sync.dma_start(few, ment_row[MENT_ROW : MENT_ROW + 1, :].unsqueeze(1).to_broadcast([1, SPREAD, V]))
-        nc.sync.dma_start(ant_ment[:], few.unsqueeze(1).to_broadcast([SPREAD, P // SPREAD, V]))
-
+        round_w(nc.scalar.copy, 0, 0, 0, 0, HALF)
+        round_w(nc.scalar.copy, 0, 0, HALF, HALF, P)
+        load_w(0, 1, 0, HALF)
+        load_w(0, 1, HALF, P)
+        gather_span_words(0, 0, S)
         quantize_w(0, 0)
-        gather_span_words(0, 0, S // 2)
-        gather_span_words(0, S // 2, S)
         for b in range(FIRST_AHEAD):
             z_pass(0, b, 0, True)
+        gather_ant_words(ant_words0, 0, 0, V)
 
-        round_w(nc.scalar.copy, 1, 0, 0, HALF)
-        round_w(nc.scalar.copy, 1, 0, HALF, P)
+        round_w(nc.scalar.copy, 1, 0, 0, 0, HALF)
+        load_w(1, 1, 0, HALF)
+        round_w(nc.scalar.copy, 1, 0, HALF, HALF, P)
+        load_w(1, 1, HALF, P)
         quantize_w(1, 0)
+        few = ment_few[0 : PACK * SPREAD : PACK, :]
+        nc.sync.dma_start(few, ment_row[MENT_ROW : MENT_ROW + 1, :].unsqueeze(1).to_broadcast([1, SPREAD, V]))
+        place_rows(ant_scales, ant_rows)
+        nc.sync.dma_start(ant_ment[:], few.unsqueeze(1).to_broadcast([SPREAD, P // SPREAD, V]))
+
         gather_span_words(1, 0, P)
         gather_span_words(1, P, 3 * P)
         gather_span_words(1, 3 * P, LATE)
 
-        round_w(nc.scalar.copy, 0, 1, 0, QUARTER)
-        round_w(nc.scalar.copy, 0, 1, QUARTER, HALF)
-        round_w(nc.scalar.copy, 0, 1, HALF, P, 0, PACK // 2)
-        round_w(nc.vector.tensor_copy, 0, 1, HALF, P, PACK // 2, PACK)
-        gather_late_words()
+        round_w(nc.scalar.copy, 0, 1, 0, 0, HALF)
+        round_w(nc.vector.tensor_copy, 0, 1, HALF, HALF, P)
+        nc.vector.tensor_copy(late_words[:], word_win[1][:].bitcast(U32).indirect(offs_sb[:, LATE // LIST_COL :]))
         quantize_w(0, 1)
-        round_w(nc.vector.tensor_copy, 1, 1, 0, HALF)
-        round_w(nc.vector.tensor_copy, 1, 1, HALF, P, 0, PACK // 2)
-        round_w(nc.vector.tensor_copy, 1, 1, HALF, P, PACK // 2, PACK)
+        round_w(nc.vector.tensor_copy, 1, 1, 0, 0, HALF)
+        round_w(nc.vector.tensor_copy, 1, 1, HALF, HALF, P, 0, PACK // 2)
+        round_w(nc.vector.tensor_copy, 1, 1, HALF, HALF, P, PACK // 2, PACK)
         quantize_w(1, 1, 0, PACK // 2)
         quantize_w(1, 1, PACK // 2, PACK)
-        gather_ant_words(1)
+        gather_ant_words(ant_words1, 1, 0, V)
 
         for b in range(BLOCKS):
             z_pass(0, b, 1, b >= FIRST_AHEAD)
@@ -262,8 +290,6 @@ def tile_picked_zcoref_sig_p_kernel(tc, x_words, x_scales, w1, ment, offs, ant, 
                 z_pass(0, b, 0, False)
             round_z(0, b)
         quantize_z(0, 0, BLOCKS)
-
-        gather_ant_words(0)
 
         for b in range(AHEAD):
             z_pass(1, b, 0, True)

@@ -31,7 +31,7 @@ BANKS = 8
 HALF = P // 2
 HALF_BYTES = PACK * PACK * HALF * 4
 AHEAD = 6
-FIRST_AHEAD = 6
+FIRST_AHEAD = 8
 ROWS_AT = P - PASSES * PASS_ROWS
 MENT_ROW = P - 1
 SPREAD = 8
@@ -46,20 +46,16 @@ def tile_picked_zcoref_sig_p_kernel(tc, x_words, x_scales, w1, ment, offs, ant, 
         buf_b = ctx.enter_context(tc.tile_pool(name="buf_b", bufs=1))
         buf_c = ctx.enter_context(tc.tile_pool(name="buf_c", bufs=1))
         buf_d = ctx.enter_context(tc.tile_pool(name="buf_d", bufs=1))
-        buf_e = ctx.enter_context(tc.tile_pool(name="buf_e", bufs=1))
-        buf_f = ctx.enter_context(tc.tile_pool(name="buf_f", bufs=1))
-        buf_g = ctx.enter_context(tc.tile_pool(name="buf_g", bufs=1))
-        buf_h = ctx.enter_context(tc.tile_pool(name="buf_h", bufs=1))
         psum = ctx.enter_context(tc.psum_pool(name="psum", bufs=BANKS))
 
         offs_sb = keep.tile([P, S // LIST_COL], U16, name="offs_sb")
         ant_sb = keep.tile([P, V // LIST_COL], U16, name="ant_sb")
-        scale_win = buf_a.tile([P, T], U8, name="scale_win", align_bytes=64, offset=0)
+        scale_win = keep.tile([P, T], U8, name="scale_win", align_bytes=64)
         word_win = [
             keep.tile([P, T], I32, name="word_win0", align_bytes=64),
-            buf_a.tile([P, T], I32, name="word_win1", align_bytes=64, offset=0),
+            buf_c.tile([P, T], I32, name="word_win1", align_bytes=64, offset=0),
         ]
-        ment_win = buf_c.tile([P, T], F32, name="ment_win", align_bytes=64, offset=0)
+        ment_win = keep.tile([P, T], F32, name="ment_win", align_bytes=64)
 
         warm = keep.tile([P, 2], F32, name="warm")
         nc.gpsimd.memset(warm[:, 0:1], 0.0)
@@ -70,14 +66,14 @@ def tile_picked_zcoref_sig_p_kernel(tc, x_words, x_scales, w1, ment, offs, ant, 
 
         w_raw = {}
         places = {
-            (0, 0, 0): (buf_h, 0),
-            (0, 0, HALF): (buf_b, HALF_BYTES),
-            (1, 0, 0): (buf_d, 0),
-            (1, 0, HALF): (buf_f, 0),
-            (0, 1, 0): (buf_h, 0),
-            (0, 1, HALF): (buf_b, HALF_BYTES),
+            (0, 0, 0): (buf_b, 0),
+            (0, 0, HALF): (buf_c, 0),
+            (1, 0, 0): (buf_a, 0),
+            (1, 0, HALF): (buf_b, 0),
+            (0, 1, 0): (buf_a, 0),
+            (0, 1, HALF): (buf_b, 0),
             (1, 1, 0): (buf_d, 0),
-            (1, 1, HALF): (buf_f, 0),
+            (1, 1, HALF): (buf_d, HALF_BYTES),
         }
 
         def load_w(o, h, first, last):
@@ -99,27 +95,27 @@ def tile_picked_zcoref_sig_p_kernel(tc, x_words, x_scales, w1, ment, offs, ant, 
             for o, h in squares
             if h == 1
         }
-        w_bf[0, 0] = buf_g.tile([P, PACK, P, PACK], BF16, name="w_bf00", align_bytes=64, offset=0)
-        w_bf[1, 0] = buf_e.tile([P, PACK, P, PACK], BF16, name="w_bf10", align_bytes=64, offset=0)
+        w_bf[0, 0] = keep.tile([P, PACK, P, PACK], BF16, name="w_bf00", align_bytes=64)
+        w_bf[1, 0] = buf_d.tile([P, PACK, P, PACK], BF16, name="w_bf10", align_bytes=64, offset=HALF_BYTES // 2)
         span_words = [keep.tile([P, S], U32, name=f"span_words{o}", align_bytes=64) for o in range(PASSES)]
         span_rows = keep.tile([P, S], U8, name="span_rows", align_bytes=64)
         ant_rows = keep.tile([P, V], U8, name="ant_rows", align_bytes=64)
         span_scales = keep.tile([P, S], U8, name="span_scales", align_bytes=64)
-        ant_scales = buf_e.tile([P, V], U8, name="ant_scales", align_bytes=64, offset=4 * V)
-        ant_words0 = buf_g.tile([P, V], U32, name="ant_words0", align_bytes=64, offset=0)
-        ant_words1 = buf_f.tile([P, V], U32, name="ant_words1", align_bytes=64, offset=S)
+        ant_scales = buf_b.tile([P, V], U8, name="ant_scales", align_bytes=64, offset=4 * V)
+        ant_words0 = keep.tile([P, V], U32, name="ant_words0", align_bytes=64)
+        ant_words1 = buf_d.tile([P, V], U32, name="ant_words1", align_bytes=64, offset=HALF_BYTES + S)
         ant_words = [ant_words0, ant_words1]
-        late_words = buf_b.tile([P, S - LATE], U32, name="late_words", align_bytes=64, offset=HALF_BYTES)
+        late_words = buf_b.tile([P, S - LATE], U32, name="late_words", align_bytes=64, offset=5 * V)
         z_codes = [keep.tile([P, S], U32, name=f"z_codes{h}", align_bytes=64) for h in range(PASSES)]
         z_scales = [
-            buf_f.tile([P, S], U8, name="z_scales0", align_bytes=64, offset=0),
+            buf_d.tile([P, S], U8, name="z_scales0", align_bytes=64, offset=HALF_BYTES),
             keep.tile([P, S], U8, name="z_scales1", align_bytes=64),
         ]
         ant_ment = keep.tile([P, V], F32, name="ant_ment", align_bytes=64)
         ment_row = keep.tile([P, V], F32, name="ment_row", align_bytes=64)
-        ment_few = buf_e.tile([P, V], F32, name="ment_few", align_bytes=64, offset=0)
+        ment_few = buf_b.tile([P, V], F32, name="ment_few", align_bytes=64, offset=0)
         z_bf = [
-            buf_h.tile([P, S, PACK], BF16, name="z_bf0", align_bytes=64, offset=0),
+            keep.tile([P, S, PACK], BF16, name="z_bf0", align_bytes=64),
             keep.tile([P, S, PACK], BF16, name="z_bf1", align_bytes=64),
         ]
         z_bank = {}
@@ -236,38 +232,35 @@ def tile_picked_zcoref_sig_p_kernel(tc, x_words, x_scales, w1, ment, offs, ant, 
             )
         nc.sync.dma_start(offs_sb[:], offs)
         nc.sync.dma_start(ant_sb[:], ant)
-        load_x(0)
-        nc.sync.dma_start(ment_win[MENT_ROW : MENT_ROW + 1, :], ment[0:1, :])
         load_w(0, 0, 0, HALF)
         load_w(0, 0, HALF, P)
+        nc.sync.dma_start(ment_win[MENT_ROW : MENT_ROW + 1, :], ment[0:1, :])
+        load_x(0)
         load_w(1, 0, 0, HALF)
-        load_w(1, 0, HALF, P)
 
         nc.vector.tensor_copy(span_rows[:], scale_win[:].indirect(offs_sb[:]))
         place_rows(span_scales, span_rows)
         nc.vector.tensor_copy(ant_rows[:], scale_win[:].indirect(ant_sb[:]))
-        load_x(1)
 
-        nc.scalar.activation(ment_row[:], ment_win[:].indirect(ant_sb[:]), COPY)
         round_w(nc.scalar.copy, 0, 0, 0, 0, HALF)
+        load_w(1, 0, HALF, P)
         round_w(nc.scalar.copy, 0, 0, HALF, HALF, P)
-        load_w(0, 1, 0, HALF)
-        load_w(0, 1, HALF, P)
-        gather_span_words(0, 0, S)
+        load_x(1)
+        nc.scalar.activation(ment_row[:], ment_win[:].indirect(ant_sb[:]), COPY)
         quantize_w(0, 0)
+        gather_span_words(0, 0, 3 * P)
+        gather_span_words(0, 3 * P, S)
         for b in range(FIRST_AHEAD):
             z_pass(0, b, 0, True)
         gather_ant_words(ant_words0, 0, 0, V)
 
         round_w(nc.scalar.copy, 1, 0, 0, 0, HALF)
-        load_w(1, 1, 0, HALF)
+        load_w(0, 1, 0, HALF)
         round_w(nc.scalar.copy, 1, 0, HALF, HALF, P)
-        load_w(1, 1, HALF, P)
+        load_w(0, 1, HALF, P)
         quantize_w(1, 0)
-        few = ment_few[0 : PACK * SPREAD : PACK, :]
-        nc.sync.dma_start(few, ment_row[MENT_ROW : MENT_ROW + 1, :].unsqueeze(1).to_broadcast([1, SPREAD, V]))
-        place_rows(ant_scales, ant_rows)
-        nc.sync.dma_start(ant_ment[:], few.unsqueeze(1).to_broadcast([SPREAD, P // SPREAD, V]))
+        load_w(1, 1, 0, HALF)
+        load_w(1, 1, HALF, P)
 
         gather_span_words(1, 0, P)
         gather_span_words(1, P, 3 * P)
@@ -276,6 +269,10 @@ def tile_picked_zcoref_sig_p_kernel(tc, x_words, x_scales, w1, ment, offs, ant, 
         round_w(nc.scalar.copy, 0, 1, 0, 0, HALF)
         round_w(nc.vector.tensor_copy, 0, 1, HALF, HALF, P)
         nc.vector.tensor_copy(late_words[:], word_win[1][:].bitcast(U32).indirect(offs_sb[:, LATE // LIST_COL :]))
+        few = ment_few[0 : PACK * SPREAD : PACK, :]
+        nc.sync.dma_start(few, ment_row[MENT_ROW : MENT_ROW + 1, :].unsqueeze(1).to_broadcast([1, SPREAD, V]))
+        place_rows(ant_scales, ant_rows)
+        nc.sync.dma_start(ant_ment[:], few.unsqueeze(1).to_broadcast([SPREAD, P // SPREAD, V]))
         quantize_w(0, 1)
         round_w(nc.vector.tensor_copy, 1, 1, 0, 0, HALF)
         round_w(nc.vector.tensor_copy, 1, 1, HALF, HALF, P, 0, PACK // 2)

@@ -299,16 +299,16 @@ def tile_picked_zcoref_sig_p_kernel(tc, x_words, x_scales, w1, ment, offs, ant, 
         for b in range(4, LAST):
             round_z(1, b)
         score_product(0)
+        score_product(1)
         close_second_half(LAST)
         round_z(1, LAST)
         add_ment(0)
-        score(1)
+        add_ment(1)
         quantize_z(1, 4, 6)
         score(2)
-        score(3)
         quantize_z(1, 6, 8)
-        for b in range(4):
+        for b in range(3):
             finish(b)
-        for b in range(4, BLOCKS):
+        for b in range(3, BLOCKS):
             score(b)
             finish(b)

@@ -36,6 +36,7 @@ ROWS_AT = P - PASSES * PASS_ROWS
 MENT_ROW = P - 1
 SPREAD = 8
 LATE = S - P
+DMA_ALIGN = 256
 
 
 def tile_picked_zcoref_sig_p_kernel(tc, x_words, x_scales, w1, ment, offs, ant, out):
@@ -50,12 +51,12 @@ def tile_picked_zcoref_sig_p_kernel(tc, x_words, x_scales, w1, ment, offs, ant, 
 
         offs_sb = keep.tile([P, S // LIST_COL], U16, name="offs_sb")
         ant_sb = keep.tile([P, V // LIST_COL], U16, name="ant_sb")
-        scale_win = keep.tile([P, T], U8, name="scale_win", align_bytes=64)
+        scale_win = keep.tile([P, T], U8, name="scale_win", align_bytes=DMA_ALIGN)
         word_win = [
-            keep.tile([P, T], I32, name="word_win0", align_bytes=64),
-            buf_c.tile([P, T], I32, name="word_win1", align_bytes=64, offset=0),
+            keep.tile([P, T], I32, name="word_win0", align_bytes=DMA_ALIGN),
+            buf_c.tile([P, T], I32, name="word_win1", align_bytes=DMA_ALIGN, offset=0),
         ]
-        ment_win = keep.tile([P, T], F32, name="ment_win", align_bytes=64)
+        ment_win = keep.tile([P, T], F32, name="ment_win", align_bytes=DMA_ALIGN)
 
         warm = keep.tile([P, 2], F32, name="warm")
         nc.gpsimd.memset(warm[:, 0:1], 0.0)
@@ -79,7 +80,7 @@ def tile_picked_zcoref_sig_p_kernel(tc, x_words, x_scales, w1, ment, offs, ant, 
         def load_w(o, h, first, last):
             pool, offset = places[o, h, first]
             w_raw[o, h, first] = pool.tile(
-                [P, PACK, PACK * (last - first)], F32, name=f"w_raw{o}{h}_{first}", align_bytes=64, offset=offset
+                [P, PACK, PACK * (last - first)], F32, name=f"w_raw{o}{h}_{first}", align_bytes=DMA_ALIGN, offset=offset
             )
             rows = w1[o * K_PASS : (o + 1) * K_PASS, h * K_PASS + PACK * first : h * K_PASS + PACK * last]
             nc.sync.dma_start(w_raw[o, h, first][:], rows.rearrange("(p j) c -> p j c", j=PACK))
@@ -98,10 +99,10 @@ def tile_picked_zcoref_sig_p_kernel(tc, x_words, x_scales, w1, ment, offs, ant, 
         w_bf[0, 0] = keep.tile([P, PACK, P, PACK], BF16, name="w_bf00", align_bytes=64)
         w_bf[1, 0] = buf_d.tile([P, PACK, P, PACK], BF16, name="w_bf10", align_bytes=64, offset=HALF_BYTES // 2)
         span_words = [keep.tile([P, S], U32, name=f"span_words{o}", align_bytes=64) for o in range(PASSES)]
-        span_rows = keep.tile([P, S], U8, name="span_rows", align_bytes=64)
-        ant_rows = keep.tile([P, V], U8, name="ant_rows", align_bytes=64)
-        span_scales = keep.tile([P, S], U8, name="span_scales", align_bytes=64)
-        ant_scales = buf_b.tile([P, V], U8, name="ant_scales", align_bytes=64, offset=4 * V)
+        span_rows = keep.tile([P, S], U8, name="span_rows", align_bytes=DMA_ALIGN)
+        ant_rows = keep.tile([P, V], U8, name="ant_rows", align_bytes=DMA_ALIGN)
+        span_scales = keep.tile([P, S], U8, name="span_scales", align_bytes=DMA_ALIGN)
+        ant_scales = buf_b.tile([P, V], U8, name="ant_scales", align_bytes=DMA_ALIGN, offset=4 * V)
         ant_words0 = keep.tile([P, V], U32, name="ant_words0", align_bytes=64)
         ant_words1 = buf_d.tile([P, V], U32, name="ant_words1", align_bytes=64, offset=HALF_BYTES + S)
         ant_words = [ant_words0, ant_words1]
@@ -111,9 +112,9 @@ def tile_picked_zcoref_sig_p_kernel(tc, x_words, x_scales, w1, ment, offs, ant, 
             buf_d.tile([P, S], U8, name="z_scales0", align_bytes=64, offset=HALF_BYTES),
             keep.tile([P, S], U8, name="z_scales1", align_bytes=64),
         ]
-        ant_ment = keep.tile([P, V], F32, name="ant_ment", align_bytes=64)
-        ment_row = keep.tile([P, V], F32, name="ment_row", align_bytes=64)
-        ment_few = buf_b.tile([P, V], F32, name="ment_few", align_bytes=64, offset=0)
+        ant_ment = keep.tile([P, V], F32, name="ant_ment", align_bytes=DMA_ALIGN)
+        ment_row = keep.tile([P, V], F32, name="ment_row", align_bytes=DMA_ALIGN)
+        ment_few = buf_b.tile([P, V], F32, name="ment_few", align_bytes=DMA_ALIGN, offset=0)
         z_bf = [
             keep.tile([P, S, PACK], BF16, name="z_bf0", align_bytes=64),
             keep.tile([P, S, PACK], BF16, name="z_bf1", align_bytes=64),
@@ -121,7 +122,7 @@ def tile_picked_zcoref_sig_p_kernel(tc, x_words, x_scales, w1, ment, offs, ant, 
         z_bank = {}
         y_bank = {}
         logit = [keep.tile([P, V], F32, name=f"logit{b}", align_bytes=64) for b in range(BLOCKS)]
-        prob = [keep.tile([P, V], F32, name=f"prob{b}", align_bytes=64) for b in range(BLOCKS)]
+        prob = [keep.tile([P, V], F32, name=f"prob{b}", align_bytes=DMA_ALIGN) for b in range(BLOCKS)]
 
         def place_rows(scales, rows):
             for q in range(QUADRANTS):

@@ -45,8 +45,8 @@ def tile_picked_zcoref_sig_p_kernel(tc, x_words, x_scales, w1, ment, offs, ant, 
         keep = ctx.enter_context(tc.tile_pool(name="keep", bufs=1))
         buf_a = ctx.enter_context(tc.tile_pool(name="buf_a", bufs=1))
         buf_b = ctx.enter_context(tc.tile_pool(name="buf_b", bufs=1))
-        buf_c = ctx.enter_context(tc.tile_pool(name="buf_c", bufs=1))
         buf_d = ctx.enter_context(tc.tile_pool(name="buf_d", bufs=1))
+        buf_c = ctx.enter_context(tc.tile_pool(name="buf_c", bufs=1))
         psum = ctx.enter_context(tc.psum_pool(name="psum", bufs=BANKS))
 
         offs_sb = keep.tile([P, S // LIST_COL], U16, name="offs_sb")
@@ -56,19 +56,18 @@ def tile_picked_zcoref_sig_p_kernel(tc, x_words, x_scales, w1, ment, offs, ant, 
             keep.tile([P, T], I32, name="word_win0", align_bytes=DMA_ALIGN),
             buf_c.tile([P, T], I32, name="word_win1", align_bytes=DMA_ALIGN, offset=0),
         ]
-        ment_win = keep.tile([P, T], F32, name="ment_win", align_bytes=DMA_ALIGN)
+        ment_win = buf_b.tile([P, T], F32, name="ment_win", align_bytes=DMA_ALIGN, offset=0)
 
         warm = keep.tile([P, 2], F32, name="warm")
         nc.gpsimd.memset(warm[:, 0:1], 0.0)
         nc.scalar.activation(warm[:, 1:2], warm[:, 0:1], SIGMOID)
 
-        nc.vector.memset(scale_win[0:ROWS_AT, :].bitcast(I32), 0)
-        nc.vector.memset(ment_win[0:MENT_ROW, :].bitcast(I32), 0)
+        nc.gpsimd.memset(scale_win[0:ROWS_AT, :].bitcast(I32), 0)
+        nc.gpsimd.memset(ment_win[0:MENT_ROW, :].bitcast(I32), 0)
 
         w_raw = {}
         places = {
-            (0, 0, 0): (buf_b, 0),
-            (0, 0, HALF): (buf_c, 0),
+            (0, 0, 0): (buf_c, 0),
             (1, 0, 0): (buf_a, 0),
             (1, 0, HALF): (buf_b, 0),
             (0, 1, 0): (buf_a, 0),
@@ -233,9 +232,8 @@ def tile_picked_zcoref_sig_p_kernel(tc, x_words, x_scales, w1, ment, offs, ant, 
             )
         nc.sync.dma_start(offs_sb[:], offs)
         nc.sync.dma_start(ant_sb[:], ant)
-        load_w(0, 0, 0, HALF)
-        load_w(0, 0, HALF, P)
         nc.sync.dma_start(ment_win[MENT_ROW : MENT_ROW + 1, :], ment[0:1, :])
+        load_w(0, 0, 0, P)
         load_x(0)
         load_w(1, 0, 0, HALF)
 
@@ -243,11 +241,11 @@ def tile_picked_zcoref_sig_p_kernel(tc, x_words, x_scales, w1, ment, offs, ant, 
         place_rows(span_scales, span_rows)
         nc.vector.tensor_copy(ant_rows[:], scale_win[:].indirect(ant_sb[:]))
 
-        round_w(nc.scalar.copy, 0, 0, 0, 0, HALF)
-        load_w(1, 0, HALF, P)
-        round_w(nc.scalar.copy, 0, 0, HALF, HALF, P)
-        load_x(1)
         nc.scalar.activation(ment_row[:], ment_win[:].indirect(ant_sb[:]), COPY)
+        load_w(1, 0, HALF, P)
+        round_w(nc.scalar.copy, 0, 0, 0, 0, 3 * P // 4)
+        round_w(nc.vector.tensor_copy, 0, 0, 0, 3 * P // 4, P)
+        load_x(1)
         quantize_w(0, 0)
         gather_span_words(0, 0, 3 * P)
         gather_span_words(0, 3 * P, S)

@@ -35,7 +35,6 @@ FIRST_AHEAD = 8
 ROWS_AT = P - PASSES * PASS_ROWS
 MENT_ROW = P - 1
 SPREAD = 8
-LATE = S - P
 DMA_ALIGN = 256
 
 
@@ -105,7 +104,6 @@ def tile_picked_zcoref_sig_p_kernel(tc, x_words, x_scales, w1, ment, offs, ant, 
         ant_words0 = keep.tile([P, V], U32, name="ant_words0", align_bytes=64)
         ant_words1 = buf_d.tile([P, V], U32, name="ant_words1", align_bytes=64, offset=HALF_BYTES + S)
         ant_words = [ant_words0, ant_words1]
-        late_words = buf_b.tile([P, S - LATE], U32, name="late_words", align_bytes=64, offset=5 * V)
         z_codes = [keep.tile([P, S], U32, name=f"z_codes{h}", align_bytes=64) for h in range(PASSES)]
         z_scales = [
             buf_d.tile([P, S], U8, name="z_scales0", align_bytes=64, offset=HALF_BYTES),
@@ -158,8 +156,6 @@ def tile_picked_zcoref_sig_p_kernel(tc, x_words, x_scales, w1, ment, offs, ant, 
                 z_bank[h, b] = psum.tile([P, PACK, P], F32, name="z_bank", tag="bank")
             spans = slice(b * P, (b + 1) * P)
             words = span_words[o][:, spans]
-            if o == 1 and b * P >= LATE:
-                words = late_words[:, b * P - LATE : (b + 1) * P - LATE]
             for r in range(PACK):
                 cols = slice(r * P, (r + 1) * P)
                 nc.tensor.matmul_mx(
@@ -263,16 +259,17 @@ def tile_picked_zcoref_sig_p_kernel(tc, x_words, x_scales, w1, ment, offs, ant, 
 
         gather_span_words(1, 0, P)
         gather_span_words(1, P, 3 * P)
-        gather_span_words(1, 3 * P, LATE)
+        gather_span_words(1, 3 * P, S)
 
         round_w(nc.scalar.copy, 0, 1, 0, 0, HALF)
-        round_w(nc.vector.tensor_copy, 0, 1, HALF, HALF, P)
-        nc.vector.tensor_copy(late_words[:], word_win[1][:].bitcast(U32).indirect(offs_sb[:, LATE // LIST_COL :]))
+        round_w(nc.vector.tensor_copy, 0, 1, HALF, HALF, P, 0, PACK // 2)
+        round_w(nc.vector.tensor_copy, 0, 1, HALF, HALF, P, PACK // 2, PACK)
         few = ment_few[0 : PACK * SPREAD : PACK, :]
         nc.sync.dma_start(few, ment_row[MENT_ROW : MENT_ROW + 1, :].unsqueeze(1).to_broadcast([1, SPREAD, V]))
         place_rows(ant_scales, ant_rows)
         nc.sync.dma_start(ant_ment[:], few.unsqueeze(1).to_broadcast([SPREAD, P // SPREAD, V]))
-        quantize_w(0, 1)
+        quantize_w(0, 1, 0, PACK // 2)
+        quantize_w(0, 1, PACK // 2, PACK)
         round_w(nc.vector.tensor_copy, 1, 1, 0, 0, HALF)
         round_w(nc.vector.tensor_copy, 1, 1, HALF, HALF, P, 0, PACK // 2)
         round_w(nc.vector.tensor_copy, 1, 1, HALF, HALF, P, PACK // 2, PACK)

from contextlib import ExitStack

import concourse.mybir as mybir

K, T, S, V = 1024, 2048, 1024, 512
FLOPS = 2 * K * K * S + 2 * K * S * V

F32 = mybir.dt.float32
BF16 = mybir.dt.bfloat16
I32 = mybir.dt.int32
U32 = mybir.dt.uint32
U16 = mybir.dt.uint16
U8 = mybir.dt.uint8
FP8X4 = mybir.dt.float8_e4m3fn_x4
SIGMOID = mybir.ActivationFunctionType.Sigmoid
COPY = mybir.ActivationFunctionType.Copy
ADD = mybir.AluOpType.add

P = 128
PACK = 4
K_PASS = P * PACK
PASSES = K // K_PASS
QUADRANTS = 4
QUADRANT = P // QUADRANTS
SCALE_ROWS = 4
PASS_ROWS = QUADRANTS * SCALE_ROWS
LIST_COL = 16
BLOCKS = S // P
LAST = BLOCKS - 1
BANKS = 8
HALF = P // 2
HALF_BYTES = PACK * PACK * HALF * 4
AHEAD = 6
FIRST_AHEAD = 8
ROWS_AT = P - PASSES * PASS_ROWS
MENT_ROW = P - 1
SPREAD = 8
DMA_ALIGN = 256


def tile_picked_zcoref_sig_p_kernel(tc, x_words, x_scales, w1, ment, offs, ant, out):
    nc = tc.nc
    with ExitStack() as ctx:
        keep = ctx.enter_context(tc.tile_pool(name="keep", bufs=1))
        buf_a = ctx.enter_context(tc.tile_pool(name="buf_a", bufs=1))
        buf_b = ctx.enter_context(tc.tile_pool(name="buf_b", bufs=1))
        buf_d = ctx.enter_context(tc.tile_pool(name="buf_d", bufs=1))
        buf_c = ctx.enter_context(tc.tile_pool(name="buf_c", bufs=1))
        psum = ctx.enter_context(tc.psum_pool(name="psum", bufs=BANKS))

        offs_sb = keep.tile([P, S // LIST_COL], U16, name="offs_sb")
        ant_sb = keep.tile([P, V // LIST_COL], U16, name="ant_sb")
        scale_win = keep.tile([P, T], U8, name="scale_win", align_bytes=DMA_ALIGN)
        word_win = [
            keep.tile([P, T], I32, name="word_win0", align_bytes=DMA_ALIGN),
            buf_c.tile([P, T], I32, name="word_win1", align_bytes=DMA_ALIGN, offset=0),
        ]
        ment_win = buf_b.tile([P, T], F32, name="ment_win", align_bytes=DMA_ALIGN, offset=0)

        warm = keep.tile([P, 2], F32, name="warm")
        nc.gpsimd.memset(warm[:, 0:1], 0.0)
        nc.scalar.activation(warm[:, 1:2], warm[:, 0:1], SIGMOID)

        nc.gpsimd.memset(scale_win[0:ROWS_AT, :].bitcast(I32), 0)
        nc.gpsimd.memset(ment_win[0:MENT_ROW, :].bitcast(I32), 0)

        w_raw = {}
        places = {
            (0, 0, 0): (buf_c, 0),
            (1, 0, 0): (buf_a, 0),
            (1, 0, HALF): (buf_b, 0),
            (0, 1, 0): (buf_a, 0),
            (0, 1, HALF): (buf_b, 0),
            (1, 1, 0): (buf_d, 0),
            (1, 1, HALF): (buf_d, HALF_BYTES),
        }

        def load_w(o, h, first, last):
            pool, offset = places[o, h, first]
            w_raw[o, h, first] = pool.tile(
                [P, PACK, PACK * (last - first)], F32, name=f"w_raw{o}{h}_{first}", align_bytes=DMA_ALIGN, offset=offset
            )
            rows = w1[o * K_PASS : (o + 1) * K_PASS, h * K_PASS + PACK * first : h * K_PASS + PACK * last]
            nc.sync.dma_start(w_raw[o, h, first][:], rows.rearrange("(p j) c -> p j c", j=PACK))

        def load_x(o):
            nc.sync.dma_start(word_win[o][:], x_words[o].rearrange("p n r -> p (n r)").bitcast(I32))

        squares = [(o, h) for h in range(PASSES) for o in range(PASSES)]
        w_codes = {(o, h): keep.tile([P, K_PASS], U32, name=f"w_codes{o}{h}", align_bytes=64) for o, h in squares}
        w_scales = {(o, h): keep.tile([P, K_PASS], U8, name=f"w_scales{o}{h}", align_bytes=64) for o, h in squares}
        w_bf = {
            (o, h): keep.tile([P, PACK, P, PACK], BF16, name=f"w_bf{o}{h}", align_bytes=64)
            for o, h in squares
            if h == 1
        }
        w_bf[0, 0] = keep.tile([P, PACK, P, PACK], BF16, name="w_bf00", align_bytes=64)
        w_bf[1, 0] = buf_d.tile([P, PACK, P, PACK], BF16, name="w_bf10", align_bytes=64, offset=HALF_BYTES // 2)
        span_words = [keep.tile([P, S], U32, name=f"span_words{o}", align_bytes=64) for o in range(PASSES)]
        span_rows = keep.tile([P, S], U8, name="span_rows", align_bytes=DMA_ALIGN)
        ant_rows = keep.tile([P, V], U8, name="ant_rows", align_bytes=DMA_ALIGN)
        span_scales = keep.tile([P, S], U8, name="span_scales", align_bytes=DMA_ALIGN)
        ant_scales = buf_b.tile([P, V], U8, name="ant_scales", align_bytes=DMA_ALIGN, offset=4 * V)
        ant_words0 = keep.tile([P, V], U32, name="ant_words0", align_bytes=64)
        ant_words1 = buf_d.tile([P, V], U32, name="ant_words1", align_bytes=64, offset=HALF_BYTES + S)
        ant_words = [ant_words0, ant_words1]
        z_codes = [keep.tile([P, S], U32, name=f"z_codes{h}", align_bytes=64) for h in range(PASSES)]
        z_scales = [
            buf_d.tile([P, S], U8, name="z_scales0", align_bytes=64, offset=HALF_BYTES),
            keep.tile([P, S], U8, name="z_scales1", align_bytes=64),
        ]
        ant_ment = keep.tile([P, V], F32, name="ant_ment", align_bytes=DMA_ALIGN)
        ment_row = keep.tile([P, V], F32, name="ment_row", align_bytes=DMA_ALIGN)
        ment_few = buf_b.tile([P, V], F32, name="ment_few", align_bytes=DMA_ALIGN, offset=0)
        z_bf = [
            keep.tile([P, S, PACK], BF16, name="z_bf0", align_bytes=64),
            keep.tile([P, S, PACK], BF16, name="z_bf1", align_bytes=64),
        ]
        z_bank = {}
        y_bank = {}
        logit = [keep.tile([P, V], F32, name=f"logit{b}", align_bytes=64) for b in range(BLOCKS)]
        prob = [keep.tile([P, V], F32, name=f"prob{b}", align_bytes=DMA_ALIGN) for b in range(BLOCKS)]

        def place_rows(scales, rows):
            for q in range(QUADRANTS):
                nc.sync.dma_start(
                    scales[QUADRANT * q : QUADRANT * q + PASSES * SCALE_ROWS, :].bitcast(I32),
                    rows[ROWS_AT + q : P : QUADRANTS, :].bitcast(I32),
                )

        def gather_span_words(o, first, last):
            entries = offs_sb[:, first // LIST_COL : last // LIST_COL]
            nc.vector.tensor_copy(span_words[o][:, first:last], word_win[o][:].bitcast(U32).indirect(entries))

        def gather_ant_words(into, o, first, last):
            entries = ant_sb[:, first // LIST_COL : last // LIST_COL]
            nc.vector.tensor_copy(into[:], word_win[o][:].bitcast(U32).indirect(entries))

        def round_w(copy, o, h, piece, first, last, r_first=0, r_last=PACK):
            raw = w_raw[o, h, piece][:].rearrange("p j (m r) -> p m j r", r=PACK)
            copy(
                w_bf[o, h][:, r_first:r_last, first:last, :].rearrange("p r m j -> p m j r"),
                raw[:, first - piece : last - piece, :, r_first:r_last],
            )

        def quantize_w(o, h, r_first=0, r_last=PACK):
            cols = slice(r_first * P, r_last * P)
            nc.vector.quantize_mx(
                out=w_codes[o, h][:, cols].bitcast(FP8X4),
                scales=w_scales[o, h][:, cols],
                in_=w_bf[o, h][:, r_first:r_last].rearrange("p r m j -> p (r m j)"),
            )

        def z_pass(h, b, o, opens):
            if opens:
                z_bank[h, b] = psum.tile([P, PACK, P], F32, name="z_bank", tag="bank")
            spans = slice(b * P, (b + 1) * P)
            words = span_words[o][:, spans]
            for r in range(PACK):
                cols = slice(r * P, (r + 1) * P)
                nc.tensor.matmul_mx(
                    out=z_bank[h, b][:, r, :],
                    lhsT=w_codes[o, h][:, cols].bitcast(FP8X4),
                    lhsT_scale=w_scales[o, h][:, cols],
                    rhs=words.bitcast(FP8X4),
                    rhs_scale=span_scales[SCALE_ROWS * o :, spans],
                    start=(opens and r == 0),
                    stop=(not opens and r == PACK - 1),
                )

        def close_second_half(b):
            z_pass(1, b, 1, b >= AHEAD)
            if b >= AHEAD:
                z_pass(1, b, 0, False)

        def round_z(h, b):
            nc.scalar.copy(z_bf[h][:, b * P : (b + 1) * P, :], z_bank[h, b][:].rearrange("p r n -> p n r"))

        def quantize_z(h, first, last):
            spans = slice(first * P, last * P)
            nc.vector.quantize_mx(
                out=z_codes[h][:, spans].bitcast(FP8X4),
                scales=z_scales[h][:, spans],
                in_=z_bf[h][:, spans, :].rearrange("p n r -> p (n r)"),
            )

        def column_runs(b):
            if b < LAST:
                return [slice(0, V)]
            return [slice(0, V // 2), slice(V // 2, V)]

        def score_pass(b, bank, h, words, cols, start, stop):
            spans = slice(b * P, (b + 1) * P)
            nc.tensor.matmul_mx(
                out=bank,
                lhsT=z_codes[h][:, spans].bitcast(FP8X4),
                lhsT_scale=z_scales[h][:, spans],
                rhs=words.bitcast(FP8X4),
                rhs_scale=ant_scales[SCALE_ROWS * h :, cols],
                start=start,
                stop=stop,
            )

        def score_product(b):
            for cols in column_runs(b):
                bank = psum.tile([P, cols.stop - cols.start], F32, name="y_bank", tag="bank")
                y_bank[b, cols.start] = bank
                for h in range(PASSES):
                    score_pass(b, bank[:], h, ant_words[h][:, cols], cols, h == 0, h == PASSES - 1)

        def add_ment(b):
            for cols in column_runs(b):
                nc.vector.tensor_tensor(logit[b][:, cols], y_bank[b, cols.start][:], ant_ment[:, cols], ADD)

        def score(b):
            score_product(b)
            add_ment(b)

        def finish(b):
            for cols in column_runs(b):
                nc.scalar.activation(prob[b][:, cols], logit[b][:, cols], SIGMOID)
            nc.sync.dma_start(out[b * P : (b + 1) * P, :], prob[b][:])

        for o in range(PASSES):
            nc.sync.dma_start(
                scale_win[ROWS_AT + PASS_ROWS * o : ROWS_AT + PASS_ROWS * (o + 1), :].bitcast(I32),
                x_scales[o].bitcast(I32).rearrange("(q r) c -> r q c", r=SCALE_ROWS),
            )
        nc.sync.dma_start(offs_sb[:], offs)
        nc.sync.dma_start(ant_sb[:], ant)
        nc.sync.dma_start(ment_win[MENT_ROW : MENT_ROW + 1, :], ment[0:1, :])
        load_w(0, 0, 0, P)
        load_x(0)
        load_w(1, 0, 0, HALF)

        nc.vector.tensor_copy(span_rows[:], scale_win[:].indirect(offs_sb[:]))
        place_rows(span_scales, span_rows)
        nc.vector.tensor_copy(ant_rows[:], scale_win[:].indirect(ant_sb[:]))

        nc.scalar.activation(ment_row[:], ment_win[:].indirect(ant_sb[:]), COPY)
        load_w(1, 0, HALF, P)
        round_w(nc.scalar.copy, 0, 0, 0, 0, 3 * P // 4)
        round_w(nc.vector.tensor_copy, 0, 0, 0, 3 * P // 4, P)
        load_x(1)
        quantize_w(0, 0)
        gather_span_words(0, 0, 3 * P)
        gather_span_words(0, 3 * P, S)
        for b in range(FIRST_AHEAD):
            z_pass(0, b, 0, True)
        gather_ant_words(ant_words0, 0, 0, V)

        round_w(nc.scalar.copy, 1, 0, 0, 0, HALF)
        load_w(0, 1, 0, HALF)
        round_w(nc.scalar.copy, 1, 0, HALF, HALF, P)
        load_w(0, 1, HALF, P)
        quantize_w(1, 0)
        load_w(1, 1, 0, HALF)
        load_w(1, 1, HALF, P)

        gather_span_words(1, 0, P)
        gather_span_words(1, P, 3 * P)
        gather_span_words(1, 3 * P, S)

        round_w(nc.scalar.copy, 0, 1, 0, 0, HALF)
        round_w(nc.vector.tensor_copy, 0, 1, HALF, HALF, P, 0, PACK // 2)
        round_w(nc.vector.tensor_copy, 0, 1, HALF, HALF, P, PACK // 2, PACK)
        few = ment_few[0 : PACK * SPREAD : PACK, :]
        nc.sync.dma_start(few, ment_row[MENT_ROW : MENT_ROW + 1, :].unsqueeze(1).to_broadcast([1, SPREAD, V]))
        place_rows(ant_scales, ant_rows)
        nc.sync.dma_start(ant_ment[:], few.unsqueeze(1).to_broadcast([SPREAD, P // SPREAD, V]))
        quantize_w(0, 1, 0, PACK // 2)
        quantize_w(0, 1, PACK // 2, PACK)
        round_w(nc.vector.tensor_copy, 1, 1, 0, 0, HALF)
        round_w(nc.vector.tensor_copy, 1, 1, HALF, HALF, P, 0, PACK // 2)
        round_w(nc.vector.tensor_copy, 1, 1, HALF, HALF, P, PACK // 2, PACK)
        quantize_w(1, 1, 0, PACK // 2)
        quantize_w(1, 1, PACK // 2, PACK)
        gather_ant_words(ant_words1, 1, 0, V)

        for b in range(BLOCKS):
            z_pass(0, b, 1, b >= FIRST_AHEAD)
            if b >= FIRST_AHEAD:
                z_pass(0, b, 0, False)
            round_z(0, b)
        quantize_z(0, 0, BLOCKS)

        for b in range(AHEAD):
            z_pass(1, b, 0, True)
        for b in range(LAST):
            close_second_half(b)
        for first in (0, 2):
            round_z(1, first)
            round_z(1, first + 1)
            quantize_z(1, first, first + 2)
        for b in range(4, LAST):
            round_z(1, b)
        score_product(0)
        score_product(1)
        close_second_half(LAST)
        round_z(1, LAST)
        add_ment(0)
        add_ment(1)
        quantize_z(1, 4, 6)
        score(2)
        quantize_z(1, 6, 8)
        for b in range(3):
            finish(b)
        for b in range(3, BLOCKS):
            score(b)
            finish(b)
